import numpy as np
import ml_dtypes


def mxq(x, axis, fmt="e4m3"):
    dtype, down = {"e4m3": (ml_dtypes.float8_e4m3fn, 7), "e5m2": (ml_dtypes.float8_e5m2, 14)}[fmt]
    v = np.moveaxis(np.asarray(x, np.float32).astype(ml_dtypes.bfloat16).astype(np.float64), axis, -1)
    blocks = v.reshape(v.shape[:-1] + (-1, 32))
    amax = np.abs(blocks).max(-1, keepdims=True)
    byte = np.maximum(np.where(amax > 0, np.frexp(amax)[1] - 1 + 127, 0) - down, 1)
    scale = np.exp2(byte - 127.0)
    codes = (blocks / scale).astype(np.float32).astype(dtype).astype(np.float64)
    return np.moveaxis((codes * scale).reshape(v.shape), -1, axis)


WIDE = False


def mx_kscale(k):
    if not WIDE:
        return np.ones(k)
    levels = np.array([10, -10, 5, -5, 0])
    if k % 512:
        return np.exp2(np.random.permutation(np.resize(levels, k // 32))).repeat(32)
    a = np.empty((k // 512, 16))
    for p in range(k // 512):
        a[p, :8] = np.random.permutation(np.resize(levels, 8))
        for g in range(8):
            far = levels[np.abs(levels - a[p, g]) >= 10]
            a[p, g + 8] = far[np.random.randint(len(far))]
    return np.exp2(a.ravel()).repeat(32)


def f64(x):
    return np.asarray(x).astype(np.float64)


def striped(idx):
    return np.tile(idx.reshape(-1, 16).T, (8, 1)).astype(np.uint16)


def unstriped(offs):
    return offs[:16].T.reshape(-1).astype(np.int64)


def striped8(idx):
    return np.concatenate([x.reshape(-1, 16).T for x in idx]).astype(np.uint16)


def runs(offs, k):
    lists = np.stack([offs[16 * r : 16 * r + 16].T.reshape(-1) for r in range(8)]).astype(np.int64)
    return lists[np.arange(k) % 512 // 64]


def pack_weight(w):
    k, n = w.shape
    w = f64(np.asarray(w, np.float32).astype(ml_dtypes.bfloat16)).reshape(k // 32, 32, n)
    amax = np.abs(w).max(1)
    byte = np.clip(np.where(amax > 0, np.frexp(amax)[1] - 1 + 127 - 7, 1), 1, 254)
    scaled = (w * np.exp2(127.0 - byte)[:, None, :]).reshape(k, n).astype(np.float32)
    words = np.ascontiguousarray(scaled.reshape(k // 512, 128, 4, n).transpose(0, 1, 3, 2)).astype(ml_dtypes.float8_e4m3fn).view(np.uint8)
    return words, np.ascontiguousarray(byte.astype(np.uint8).reshape(k // 512, 16, n))


def unpack_weight(words, scales):
    g, p, n, _ = words.shape
    vals = np.ascontiguousarray(words).view(ml_dtypes.float8_e4m3fn).astype(np.float64) * np.repeat(np.exp2(scales.astype(np.float64) - 127.0), 8, axis=1)[..., None]
    return vals.transpose(0, 1, 3, 2).reshape(g * 512, n)


def gelu(v):
    return 0.5 * v * (1.0 + np.tanh(np.sqrt(2.0 / np.pi) * (v + 0.044715 * v**3)))


K, T, S, V, N, H = 512, 2048, 512, 256, 512, 512


def setup_inputs():
    n = np.random.standard_normal
    s = mx_kscale(K)[:, None]
    u = mx_kscale(H)
    packed_xT = pack_weight(n((K, T)) * s)
    return {
        "x_words": packed_xT[0],
        "x_scales": packed_xT[1],
        "w1": (n((K, H)) / np.sqrt(K) / s * u).astype(np.float32),
        "wt": np.repeat(np.random.uniform(0.3, 1.2, (8, V)), 64, axis=0).astype(np.float32),
        "w2": (n((H, N)) / np.sqrt(H) / u[:, None]).astype(np.float32),
        "offs": striped(np.random.permutation(T)[:S]),
        "take": striped8(np.stack([np.random.permutation(S)[:V] for _ in range(8)])),
    }


def reference(x_words, x_scales, w1, wt, w2, offs, take):
    xq = unpack_weight(x_words, x_scales)[:, unstriped(offs)]
    y = mxq(f64(w1), 0, "e4m3").T @ xq
    e = (gelu(y[np.arange(H)[:, None], runs(take, H)])) * f64(wt)
    z = y.copy()
    z[np.arange(H)[:, None], runs(take, H)] = e
    return mxq(f64(w2), 0, "e4m3").T @ mxq(z, 0, "e4m3")

@@ -1,0 +1,191 @@
+from contextlib import ExitStack
+
+import concourse.mybir as mybir
+
+K, T, S, V, N, H = 512, 2048, 512, 256, 512, 512
+
+FLOPS = 2 * K * H * S + 2 * H * N * S
+BYTES = K * T + K * T // 32 + 4 * (K * H + H * N + 8 * V + N * S) + 2 * 128 * (S + V) // 16
+
+F32 = mybir.dt.float32
+BF16 = mybir.dt.bfloat16
+I32 = mybir.dt.int32
+U32 = mybir.dt.uint32
+U16 = mybir.dt.uint16
+U8 = mybir.dt.uint8
+FP8X4 = mybir.dt.float8_e4m3fn_x4
+GELU = mybir.ActivationFunctionType.Gelu_apprx_tanh
+MULT = mybir.AluOpType.mult
+
+P = 128
+PACK = 4
+HALF = S // 2
+ORDER = (1, 3, 0, 2)
+CHUNKS = ((0, 128), (128, 256), (256, 512))
+
+
+def tile_picked_modtrue_gelu_p_kernel(tc, x_words, x_scales, w1, wt, w2, offs, take, out):
+    nc = tc.nc
+    with ExitStack() as ctx:
+        lists = ctx.enter_context(tc.tile_pool(name="lists", bufs=1))
+        keep = ctx.enter_context(tc.tile_pool(name="keep", bufs=1))
+        psum = ctx.enter_context(tc.psum_pool(name="psum", bufs=8))
+
+        offs_sb = lists.tile([P, S // 16], U16, name="offs_sb")
+        take_sb = lists.tile([P, V // 16], U16, name="take_sb")
+
+        scale_table = keep.tile([P, T], U8, name="scale_table", align_bytes=64)
+        nc.vector.memset(scale_table[:].bitcast(I32), 0)
+        nc.sync.dma_start(offs_sb[:], offs)
+        w1_raw = keep.tile([P, PACK, H], F32, name="w1_raw")
+        nc.sync.dma_start(w1_raw[:], w1.rearrange("(p j) c -> p j c", j=PACK))
+        for q in range(4):
+            nc.sync.dma_start(scale_table[32 * q : 32 * q + 4, :].bitcast(I32), x_scales[0, 4 * q : 4 * q + 4, :].bitcast(I32))
+        word_table = keep.tile([P, T], U32, name="word_table", align_bytes=64)
+        nc.sync.dma_start(word_table[:].bitcast(I32), x_words[0].rearrange("p n r -> p (n r)").bitcast(I32))
+        nc.sync.dma_start(take_sb[:], take)
+        wt_sb = keep.tile([P, V], F32, name="wt_sb", tag="wt_then_w2_codes", align_bytes=64)
+        nc.sync.dma_start(wt_sb[:], wt.rearrange("(p j) v -> p j v", j=PACK)[:, 0, :])
+
+        w2_raw = keep.tile([P, PACK, N], F32, name="w2_raw")
+        nc.sync.dma_start(w2_raw[:], w2.rearrange("(p j) c -> p j c", j=PACK))
+
+        w1_grouped = keep.tile([P, PACK, P, PACK], BF16, name="w1_grouped", align_bytes=64)
+        for copy, ms in ((nc.vector.tensor_copy, slice(0, P // 2)), (nc.scalar.copy, slice(P // 2, P))):
+            copy(
+                w1_grouped[:].rearrange("p t m j -> p m t j")[:, ms],
+                w1_raw[:].rearrange("p j (m t) -> p m t j", t=PACK)[:, ms],
+            )
+
+        x_scale = keep.tile([P, S], U8, name="x_scale", align_bytes=64)
+        nc.vector.tensor_copy(x_scale[:], scale_table[:].indirect(offs_sb[:]))
+        w1_codes = keep.tile([P, H], U32, name="w1_codes", align_bytes=64)
+        w1_scale = keep.tile([P, H], U8, name="w1_scale", align_bytes=64)
+        nc.vector.quantize_mx(w1_codes[:].bitcast(FP8X4), w1_scale[:], w1_grouped[:].rearrange("p t m j -> p (t m j)"))
+
+        x_codes = keep.tile([P, S], U32, name="x_codes", align_bytes=64)
+        for h in range(2):
+            nc.vector.tensor_copy(
+                x_codes[:, h * HALF : (h + 1) * HALF], word_table[:].indirect(offs_sb[:, h * HALF // 16 : (h + 1) * HALF // 16])
+            )
+
+        def first(t, dest, cols):
+            nc.tensor.matmul_mx(
+                dest,
+                lhsT=w1_codes[:, t * P : (t + 1) * P].bitcast(FP8X4),
+                lhsT_scale=w1_scale[:, t * P : (t + 1) * P],
+                rhs=x_codes[:, cols].bitcast(FP8X4),
+                rhs_scale=x_scale[:, cols],
+                start=True,
+                stop=True,
+            )
+
+        halves = [slice(h * HALF, (h + 1) * HALF) for h in range(2)]
+        y = {}
+        y[ORDER[0]] = [(psum.tile([P, S], F32, name="bank")[:, 0:HALF], cols) for cols in halves]
+        for t in ORDER[1:]:
+            y[t] = [(psum.tile([P, S], F32, name="bank")[:], slice(0, S))]
+        for h in range(2):
+            first(ORDER[0], y[ORDER[0]][h][0], halves[h])
+            first(ORDER[1], y[ORDER[1]][0][0][:, halves[h]], halves[h])
+        for t in ORDER[2:]:
+            first(t, y[t][0][0], slice(0, S))
+
+        picked = {}
+        for t in ORDER:
+            act = keep.tile([P, S], F32, name="act", tag="row", bufs=4)
+            for part, cols in y[t]:
+                nc.scalar.activation(act[:, cols], part, GELU)
+            picked[t] = keep.tile([P, V], F32, name=f"picked{t}")
+            nc.vector.tensor_copy(picked[t][:], act[:].indirect(take_sb[:]))
+
+        pairs = [keep.tile([P, 2, S], F32, name=f"pair{u}") for u in range(2)]
+        window = {}
+        for t in ORDER:
+            if t % 2:
+                single = keep.tile([P, S], F32, name="single", tag="row", bufs=4)
+                window[t] = single[:]
+            else:
+                window[t] = pairs[t // 2][:].rearrange("p s c -> p (s c)")
+            for part, cols in y[t]:
+                nc.scalar.copy(window[t][:, cols], part)
+
+        w2_grouped = keep.tile([P, N, PACK], BF16, name="w2_grouped", align_bytes=64)
+
+        def group_w2(mt):
+            cols = slice(mt * P, (mt + 1) * P)
+            nc.scalar.copy(
+                w2_grouped[:, cols, :].rearrange("p (c i) j -> p c j i", i=4),
+                w2_raw[:, :, cols].rearrange("p j (c i) -> p c j i", i=4),
+            )
+
+        def scatter(t):
+            nc.vector.tensor_tensor(window[t].indirect(take_sb[:]), picked[t][:], wt_sb[:], MULT)
+
+        z_grouped = [keep.tile([P, b - a, PACK], BF16, name=f"z_grouped{a}", align_bytes=64) for a, b in CHUNKS]
+
+        def group_z(copy, u, c):
+            a, b = CHUNKS[c]
+            copy(z_grouped[c][:, :, 2 * u : 2 * u + 2], pairs[u][:, :, a:b].rearrange("p s c -> p c s"))
+
+        scatter(1)
+        scatter(3)
+        group_w2(0)
+        nc.scalar.copy(pairs[0][:, 1, :], window[1])
+        scatter(0)
+        group_w2(1)
+        group_w2(2)
+        nc.scalar.copy(pairs[1][:, 1, :], window[3])
+        scatter(2)
+        group_w2(3)
+        for c in range(len(CHUNKS)):
+            group_z(nc.scalar.copy, 0, c)
+
+        w2_codes = keep.tile([P, N], U32, name="w2_codes", tag="wt_then_w2_codes", align_bytes=64)
+        w2_scale = keep.tile([P, N], U8, name="w2_scale", align_bytes=64)
+
+        def quantize_w2(half):
+            cols = slice(half * N // 2, (half + 1) * N // 2)
+            nc.vector.quantize_mx(
+                w2_codes[:, cols].bitcast(FP8X4), w2_scale[:, cols], w2_grouped[:, cols, :].rearrange("p c j -> p (c j)")
+            )
+
+        z_codes = [keep.tile([P, b - a], U32, name=f"z_codes{a}", align_bytes=64) for a, b in CHUNKS]
+        z_scale = [keep.tile([P, b - a], U8, name=f"z_scale{a}", align_bytes=64) for a, b in CHUNKS]
+
+        def quantize_z(c):
+            nc.vector.quantize_mx(z_codes[c][:].bitcast(FP8X4), z_scale[c][:], z_grouped[c][:].rearrange("p c j -> p (c j)"))
+
+        out_rows = out.rearrange("(mt p) j -> p mt j", p=P)
+
+        def second(c, mts, copy):
+            a, b = CHUNKS[c]
+            bank = psum.tile([P, S], F32, name="bank")
+            for i, mt in enumerate(mts):
+                nc.tensor.matmul_mx(
+                    bank[:, i * (b - a) : (i + 1) * (b - a)],
+                    lhsT=w2_codes[:, mt * P : (mt + 1) * P].bitcast(FP8X4),
+                    lhsT_scale=w2_scale[:, mt * P : (mt + 1) * P],
+                    rhs=z_codes[c][:].bitcast(FP8X4),
+                    rhs_scale=z_scale[c][:],
+                    start=True,
+                    stop=True,
+                )
+            staged = keep.tile([P, len(mts), b - a], F32, name=f"staged{c}{mts[0]}")
+            copy(staged[:].rearrange("p i c -> p (i c)"), bank[:, 0 : len(mts) * (b - a)])
+            nc.sync.dma_start(out_rows[:, mts[0] : mts[-1] + 1, a:b], staged[:])
+
+        group_z(nc.vector.tensor_copy, 1, 0)
+        quantize_w2(0)
+        quantize_z(0)
+        second(0, (0, 1), nc.scalar.copy)
+        group_z(nc.vector.tensor_copy, 1, 1)
+        quantize_w2(1)
+        second(0, (2, 3), nc.scalar.copy)
+        quantize_z(1)
+        second(1, (0, 1), nc.scalar.copy)
+        second(1, (2, 3), nc.scalar.copy)
+        group_z(nc.vector.tensor_copy, 1, 2)
+        quantize_z(2)
+        for mt in range(4):
+            second(2, (mt,), nc.vector.tensor_copy if mt % 2 else nc.scalar.copy)

@@ -34,46 +34,53 @@ def tile_picked_modtrue_gelu_p_kernel(tc, x_words, x_scales, w1, wt, w2, offs, t
         offs_sb = lists.tile([P, S // 16], U16, name="offs_sb")
         take_sb = lists.tile([P, V // 16], U16, name="take_sb")
 
-        scale_table = keep.tile([P, T], U8, name="scale_table", align_bytes=64)
+        scale_table = keep.tile([P, T], U8, name="scale_table", tag="table_then_w1", align_bytes=64)
         nc.vector.memset(scale_table[:].bitcast(I32), 0)
+        x_scale = keep.tile([P, S], U8, name="x_scale", align_bytes=64)
+        nc.vector.memset(x_scale[:].bitcast(I32), 0)
+        nc.scalar.dma_start(scale_table[0:P:8, :].bitcast(I32), x_scales[0].bitcast(I32))
         nc.sync.dma_start(offs_sb[:], offs)
-        w1_raw = keep.tile([P, PACK, H], F32, name="w1_raw")
+        w1_raw = keep.tile([P, PACK, H], F32, name="w1_raw", tag="w_raw")
         nc.sync.dma_start(w1_raw[:], w1.rearrange("(p j) c -> p j c", j=PACK))
-        for q in range(4):
-            nc.sync.dma_start(scale_table[32 * q : 32 * q + 4, :].bitcast(I32), x_scales[0, 4 * q : 4 * q + 4, :].bitcast(I32))
+        nc.sync.dma_start(take_sb[:], take)
         word_table = keep.tile([P, T], U32, name="word_table", align_bytes=64)
         nc.sync.dma_start(word_table[:].bitcast(I32), x_words[0].rearrange("p n r -> p (n r)").bitcast(I32))
-        nc.sync.dma_start(take_sb[:], take)
-        wt_sb = keep.tile([P, V], F32, name="wt_sb", tag="wt_then_w2_codes", align_bytes=64)
-        nc.sync.dma_start(wt_sb[:], wt.rearrange("(p j) v -> p j v", j=PACK)[:, 0, :])
 
-        w2_raw = keep.tile([P, PACK, N], F32, name="w2_raw")
-        nc.sync.dma_start(w2_raw[:], w2.rearrange("(p j) c -> p j c", j=PACK))
+        picked_scale = keep.tile([P, S], U8, name="picked_scale", tag="scale_wt_w2", align_bytes=64)
+        nc.vector.tensor_copy(picked_scale[:], scale_table[:].indirect(offs_sb[:]))
+        for q in range(4):
+            nc.sync.dma_start(x_scale[32 * q : 32 * q + 4, :].bitcast(I32), picked_scale[32 * q : 32 * q + 32 : 8, :].bitcast(I32))
 
-        w1_grouped = keep.tile([P, PACK, P, PACK], BF16, name="w1_grouped", align_bytes=64)
-        for copy, ms in ((nc.vector.tensor_copy, slice(0, P // 2)), (nc.scalar.copy, slice(P // 2, P))):
-            copy(
-                w1_grouped[:].rearrange("p t m j -> p m t j")[:, ms],
-                w1_raw[:].rearrange("p j (m t) -> p m t j", t=PACK)[:, ms],
+        w1_grouped = keep.tile([P, 2, 2, P, PACK], BF16, name="w1_grouped", tag="table_then_w1", align_bytes=64)
+        for e in (1, 0):
+            nc.vector.tensor_copy(
+                w1_grouped[:, e].rearrange("p u m j -> p m u j"),
+                w1_raw[:].rearrange("p j (m u e) -> p e m u j", u=2, e=2)[:, e],
             )
-
-        x_scale = keep.tile([P, S], U8, name="x_scale", align_bytes=64)
-        nc.vector.tensor_copy(x_scale[:], scale_table[:].indirect(offs_sb[:]))
+        w2_raw = keep.tile([P, PACK, N], F32, name="w2_raw", tag="w_raw")
+        nc.sync.dma_start(w2_raw[:], w2.rearrange("(p j) c -> p j c", j=PACK))
+        wt_sb = keep.tile([P, V], F32, name="wt_sb", tag="scale_wt_w2", align_bytes=64)
+        nc.sync.dma_start(wt_sb[:], wt.rearrange("(p j) v -> p j v", j=PACK)[:, 0, :])
         w1_codes = keep.tile([P, H], U32, name="w1_codes", align_bytes=64)
         w1_scale = keep.tile([P, H], U8, name="w1_scale", align_bytes=64)
-        nc.vector.quantize_mx(w1_codes[:].bitcast(FP8X4), w1_scale[:], w1_grouped[:].rearrange("p t m j -> p (t m j)"))
+        for e in (1, 0):
+            cols = slice(e * H // 2, (e + 1) * H // 2)
+            nc.vector.quantize_mx(
+                w1_codes[:, cols].bitcast(FP8X4), w1_scale[:, cols], w1_grouped[:, e].rearrange("p u m j -> p (u m j)")
+            )
 
-        x_codes = keep.tile([P, S], U32, name="x_codes", align_bytes=64)
+        x_codes = keep.tile([P, S], U32, name="x_codes", tag="table_then_w1", align_bytes=64)
         for h in range(2):
             nc.vector.tensor_copy(
                 x_codes[:, h * HALF : (h + 1) * HALF], word_table[:].indirect(offs_sb[:, h * HALF // 16 : (h + 1) * HALF // 16])
             )
 
         def first(t, dest, cols):
+            at = (2 * (t % 2) + t // 2) * P
             nc.tensor.matmul_mx(
                 dest,
-                lhsT=w1_codes[:, t * P : (t + 1) * P].bitcast(FP8X4),
-                lhsT_scale=w1_scale[:, t * P : (t + 1) * P],
+                lhsT=w1_codes[:, at : at + P].bitcast(FP8X4),
+                lhsT_scale=w1_scale[:, at : at + P],
                 rhs=x_codes[:, cols].bitcast(FP8X4),
                 rhs_scale=x_scale[:, cols],
                 start=True,
@@ -141,7 +148,7 @@ def tile_picked_modtrue_gelu_p_kernel(tc, x_words, x_scales, w1, wt, w2, offs, t
         for c in range(len(CHUNKS)):
             group_z(nc.scalar.copy, 0, c)
 
-        w2_codes = keep.tile([P, N], U32, name="w2_codes", tag="wt_then_w2_codes", align_bytes=64)
+        w2_codes = keep.tile([P, N], U32, name="w2_codes", tag="scale_wt_w2", align_bytes=64)
         w2_scale = keep.tile([P, N], U8, name="w2_scale", align_bytes=64)
 
         def quantize_w2(half):
@@ -158,34 +165,36 @@ def tile_picked_modtrue_gelu_p_kernel(tc, x_words, x_scales, w1, wt, w2, offs, t
 
         out_rows = out.rearrange("(mt p) j -> p mt j", p=P)
 
-        def second(c, mts, copy):
-            a, b = CHUNKS[c]
+        def second(chunks, mts, copy):
+            a, b = CHUNKS[chunks[0]][0], CHUNKS[chunks[-1]][1]
             bank = psum.tile([P, S], F32, name="bank")
             for i, mt in enumerate(mts):
-                nc.tensor.matmul_mx(
-                    bank[:, i * (b - a) : (i + 1) * (b - a)],
-                    lhsT=w2_codes[:, mt * P : (mt + 1) * P].bitcast(FP8X4),
-                    lhsT_scale=w2_scale[:, mt * P : (mt + 1) * P],
-                    rhs=z_codes[c][:].bitcast(FP8X4),
-                    rhs_scale=z_scale[c][:],
-                    start=True,
-                    stop=True,
-                )
-            staged = keep.tile([P, len(mts), b - a], F32, name=f"staged{c}{mts[0]}")
+                for c in chunks:
+                    start = i * (b - a) + CHUNKS[c][0] - a
+                    nc.tensor.matmul_mx(
+                        bank[:, start : start + CHUNKS[c][1] - CHUNKS[c][0]],
+                        lhsT=w2_codes[:, mt * P : (mt + 1) * P].bitcast(FP8X4),
+                        lhsT_scale=w2_scale[:, mt * P : (mt + 1) * P],
+                        rhs=z_codes[c][:].bitcast(FP8X4),
+                        rhs_scale=z_scale[c][:],
+                        start=True,
+                        stop=True,
+                    )
+            staged = keep.tile([P, len(mts), b - a], F32, name=f"staged{a}{mts[0]}")
             copy(staged[:].rearrange("p i c -> p (i c)"), bank[:, 0 : len(mts) * (b - a)])
             nc.sync.dma_start(out_rows[:, mts[0] : mts[-1] + 1, a:b], staged[:])
 
         group_z(nc.vector.tensor_copy, 1, 0)
+        group_z(nc.scalar.copy, 1, 2)
         quantize_w2(0)
         quantize_z(0)
-        second(0, (0, 1), nc.scalar.copy)
+        second((0,), (0, 1), nc.scalar.copy)
         group_z(nc.vector.tensor_copy, 1, 1)
         quantize_w2(1)
-        second(0, (2, 3), nc.scalar.copy)
+        second((0,), (2, 3), nc.scalar.copy)
         quantize_z(1)
-        second(1, (0, 1), nc.scalar.copy)
-        second(1, (2, 3), nc.scalar.copy)
-        group_z(nc.vector.tensor_copy, 1, 2)
         quantize_z(2)
+        second((1,), (0, 1), nc.scalar.copy)
+        second((1,), (2, 3), nc.vector.tensor_copy)
         for mt in range(4):
-            second(2, (mt,), nc.vector.tensor_copy if mt % 2 else nc.scalar.copy)
+            second((2,), (mt,), nc.vector.tensor_copy if mt % 2 else nc.scalar.copy)

@@ -35,21 +35,22 @@ def tile_picked_modtrue_gelu_p_kernel(tc, x_words, x_scales, w1, wt, w2, offs, t
         take_sb = lists.tile([P, V // 16], U16, name="take_sb")
 
         scale_table = keep.tile([P, T], U8, name="scale_table", tag="table_then_w1", align_bytes=64)
-        nc.vector.memset(scale_table[:].bitcast(I32), 0)
+        for a, b in ((0, 16), (32, 64), (64, P)):
+            nc.vector.memset(scale_table[a:b, :].bitcast(I32), 0)
         x_scale = keep.tile([P, S], U8, name="x_scale", align_bytes=64)
         nc.vector.memset(x_scale[:].bitcast(I32), 0)
-        nc.scalar.dma_start(scale_table[0:P:8, :].bitcast(I32), x_scales[0].bitcast(I32))
+        nc.sync.dma_start(scale_table[16:32, :].bitcast(I32), x_scales[0].bitcast(I32))
         nc.sync.dma_start(offs_sb[:], offs)
         w1_raw = keep.tile([P, PACK, H], F32, name="w1_raw", tag="w_raw")
         nc.sync.dma_start(w1_raw[:], w1.rearrange("(p j) c -> p j c", j=PACK))
-        nc.sync.dma_start(take_sb[:], take)
         word_table = keep.tile([P, T], U32, name="word_table", align_bytes=64)
         nc.sync.dma_start(word_table[:].bitcast(I32), x_words[0].rearrange("p n r -> p (n r)").bitcast(I32))
+        nc.sync.dma_start(take_sb[:], take)
 
         picked_scale = keep.tile([P, S], U8, name="picked_scale", tag="scale_wt_w2", align_bytes=64)
         nc.vector.tensor_copy(picked_scale[:], scale_table[:].indirect(offs_sb[:]))
         for q in range(4):
-            nc.sync.dma_start(x_scale[32 * q : 32 * q + 4, :].bitcast(I32), picked_scale[32 * q : 32 * q + 32 : 8, :].bitcast(I32))
+            nc.sync.dma_start(x_scale[32 * q : 32 * q + 4, :].bitcast(I32), picked_scale[16 + 4 * q : 20 + 4 * q, :].bitcast(I32))
 
         w1_grouped = keep.tile([P, 2, 2, P, PACK], BF16, name="w1_grouped", tag="table_then_w1", align_bytes=64)
         for e in (1, 0):

@@ -43,7 +43,7 @@ def tile_picked_modtrue_gelu_p_kernel(tc, x_words, x_scales, w1, wt, w2, offs, t
         nc.sync.dma_start(offs_sb[:], offs)
         w1_raw = keep.tile([P, PACK, H], F32, name="w1_raw", tag="w_raw")
         nc.sync.dma_start(w1_raw[:], w1.rearrange("(p j) c -> p j c", j=PACK))
-        word_table = keep.tile([P, T], U32, name="word_table", align_bytes=64)
+        word_table = keep.tile([P, T], U32, name="word_table", tag="words_then_w1", align_bytes=64)
         nc.sync.dma_start(word_table[:].bitcast(I32), x_words[0].rearrange("p n r -> p (n r)").bitcast(I32))
         nc.sync.dma_start(take_sb[:], take)
 
@@ -52,36 +52,41 @@ def tile_picked_modtrue_gelu_p_kernel(tc, x_words, x_scales, w1, wt, w2, offs, t
         for q in range(4):
             nc.sync.dma_start(x_scale[32 * q : 32 * q + 4, :].bitcast(I32), picked_scale[16 + 4 * q : 20 + 4 * q, :].bitcast(I32))
 
-        w1_grouped = keep.tile([P, 2, 2, P, PACK], BF16, name="w1_grouped", tag="table_then_w1", align_bytes=64)
+        w1_grouped = {
+            1: keep.tile([P, 2, P, PACK], BF16, name="w1_grouped_odd", tag="table_then_w1", align_bytes=64),
+            0: keep.tile([P, 2, P, PACK], BF16, name="w1_grouped_even", align_bytes=64),
+        }
         for e in (1, 0):
             nc.vector.tensor_copy(
-                w1_grouped[:, e].rearrange("p u m j -> p m u j"),
+                w1_grouped[e][:].rearrange("p u m j -> p m u j"),
                 w1_raw[:].rearrange("p j (m u e) -> p e m u j", u=2, e=2)[:, e],
             )
         w2_raw = keep.tile([P, PACK, N], F32, name="w2_raw", tag="w_raw")
         nc.sync.dma_start(w2_raw[:], w2.rearrange("(p j) c -> p j c", j=PACK))
         wt_sb = keep.tile([P, V], F32, name="wt_sb", tag="scale_wt_w2", align_bytes=64)
         nc.sync.dma_start(wt_sb[:], wt.rearrange("(p j) v -> p j v", j=PACK)[:, 0, :])
-        w1_codes = keep.tile([P, H], U32, name="w1_codes", align_bytes=64)
-        w1_scale = keep.tile([P, H], U8, name="w1_scale", align_bytes=64)
-        for e in (1, 0):
-            cols = slice(e * H // 2, (e + 1) * H // 2)
-            nc.vector.quantize_mx(
-                w1_codes[:, cols].bitcast(FP8X4), w1_scale[:, cols], w1_grouped[:, e].rearrange("p u m j -> p (u m j)")
-            )
+        w1_codes, w1_scale = {}, {}
+
+        def quantize_w1(e, tag):
+            w1_codes[e] = keep.tile([P, H // 2], U32, name=f"w1_codes{e}", tag=tag, align_bytes=64)
+            w1_scale[e] = keep.tile([P, H // 2], U8, name=f"w1_scale{e}", align_bytes=64)
+            nc.vector.quantize_mx(w1_codes[e][:].bitcast(FP8X4), w1_scale[e][:], w1_grouped[e][:].rearrange("p u m j -> p (u m j)"))
+
+        quantize_w1(1, "w1_codes_odd")
 
         x_codes = keep.tile([P, S], U32, name="x_codes", tag="table_then_w1", align_bytes=64)
         for h in range(2):
             nc.vector.tensor_copy(
                 x_codes[:, h * HALF : (h + 1) * HALF], word_table[:].indirect(offs_sb[:, h * HALF // 16 : (h + 1) * HALF // 16])
             )
+        quantize_w1(0, "words_then_w1")
 
         def first(t, dest, cols):
-            at = (2 * (t % 2) + t // 2) * P
+            at = (t // 2) * P
             nc.tensor.matmul_mx(
                 dest,
-                lhsT=w1_codes[:, at : at + P].bitcast(FP8X4),
-                lhsT_scale=w1_scale[:, at : at + P],
+                lhsT=w1_codes[t % 2][:, at : at + P].bitcast(FP8X4),
+                lhsT_scale=w1_scale[t % 2][:, at : at + P],
                 rhs=x_codes[:, cols].bitcast(FP8X4),
                 rhs_scale=x_scale[:, cols],
                 start=True,
@@ -100,23 +105,18 @@ def tile_picked_modtrue_gelu_p_kernel(tc, x_words, x_scales, w1, wt, w2, offs, t
             first(t, y[t][0][0], slice(0, S))
 
         picked = {}
-        for t in ORDER:
-            act = keep.tile([P, S], F32, name="act", tag="row", bufs=4)
-            for part, cols in y[t]:
-                nc.scalar.activation(act[:, cols], part, GELU)
+
+        def pick(t):
+            act = keep.tile([P, S], F32, name=f"act{t}")
+            nc.scalar.activation(act[:], y[t][0][0], GELU)
             picked[t] = keep.tile([P, V], F32, name=f"picked{t}")
             nc.vector.tensor_copy(picked[t][:], act[:].indirect(take_sb[:]))
 
         pairs = [keep.tile([P, 2, S], F32, name=f"pair{u}") for u in range(2)]
         window = {}
-        for t in ORDER:
-            if t % 2:
-                single = keep.tile([P, S], F32, name="single", tag="row", bufs=4)
-                window[t] = single[:]
-            else:
-                window[t] = pairs[t // 2][:].rearrange("p s c -> p (s c)")
-            for part, cols in y[t]:
-                nc.scalar.copy(window[t][:, cols], part)
+        for u in range(2):
+            window[2 * u] = pairs[u][:].rearrange("p s c -> p (s c)")
+            window[2 * u + 1] = keep.tile([P, S], F32, name=f"single{u}")[:]
 
         w2_grouped = keep.tile([P, N, PACK], BF16, name="w2_grouped", align_bytes=64)
 
@@ -136,7 +136,18 @@ def tile_picked_modtrue_gelu_p_kernel(tc, x_words, x_scales, w1, wt, w2, offs, t
             a, b = CHUNKS[c]
             copy(z_grouped[c][:, :, 2 * u : 2 * u + 2], pairs[u][:, :, a:b].rearrange("p s c -> p c s"))
 
+        for part, cols in y[1]:
+            nc.vector.tensor_copy(window[1][:, cols], part)
+        raw = keep.tile([P, V], F32, name="raw")
+        nc.vector.tensor_copy(raw[:], window[1].indirect(take_sb[:]))
+        pick(3)
+        pick(0)
+        picked[1] = keep.tile([P, V], F32, name="picked1")
+        nc.scalar.activation(picked[1][:], raw[:], GELU)
         scatter(1)
+        pick(2)
+        for t in (3, 0, 2):
+            nc.scalar.copy(window[t][:, 0:S], y[t][0][0])
         scatter(3)
         group_w2(0)
         nc.scalar.copy(pairs[0][:, 1, :], window[1])
@@ -186,11 +197,11 @@ def tile_picked_modtrue_gelu_p_kernel(tc, x_words, x_scales, w1, wt, w2, offs, t
             nc.sync.dma_start(out_rows[:, mts[0] : mts[-1] + 1, a:b], staged[:])
 
         group_z(nc.vector.tensor_copy, 1, 0)
+        group_z(nc.scalar.copy, 1, 1)
         group_z(nc.scalar.copy, 1, 2)
         quantize_w2(0)
         quantize_z(0)
         second((0,), (0, 1), nc.scalar.copy)
-        group_z(nc.vector.tensor_copy, 1, 1)
         quantize_w2(1)
         second((0,), (2, 3), nc.scalar.copy)
         quantize_z(1)

@@ -157,7 +157,7 @@ def tile_picked_modtrue_gelu_p_kernel(tc, x_words, x_scales, w1, wt, w2, offs, t
         nc.scalar.copy(pairs[1][:, 1, :], window[3])
         scatter(2)
         group_w2(3)
-        for c in range(len(CHUNKS)):
+        for c in (0, 2, 1):
             group_z(nc.scalar.copy, 0, c)
 
         w2_codes = keep.tile([P, N], U32, name="w2_codes", tag="scale_wt_w2", align_bytes=64)
@@ -177,36 +177,43 @@ def tile_picked_modtrue_gelu_p_kernel(tc, x_words, x_scales, w1, wt, w2, offs, t
 
         out_rows = out.rearrange("(mt p) j -> p mt j", p=P)
 
-        def second(chunks, mts, copy):
-            a, b = CHUNKS[chunks[0]][0], CHUNKS[chunks[-1]][1]
+        def second(c, mts, dest, copy):
+            width = CHUNKS[c][1] - CHUNKS[c][0]
             bank = psum.tile([P, S], F32, name="bank")
             for i, mt in enumerate(mts):
-                for c in chunks:
-                    start = i * (b - a) + CHUNKS[c][0] - a
-                    nc.tensor.matmul_mx(
-                        bank[:, start : start + CHUNKS[c][1] - CHUNKS[c][0]],
-                        lhsT=w2_codes[:, mt * P : (mt + 1) * P].bitcast(FP8X4),
-                        lhsT_scale=w2_scale[:, mt * P : (mt + 1) * P],
-                        rhs=z_codes[c][:].bitcast(FP8X4),
-                        rhs_scale=z_scale[c][:],
-                        start=True,
-                        stop=True,
-                    )
-            staged = keep.tile([P, len(mts), b - a], F32, name=f"staged{a}{mts[0]}")
-            copy(staged[:].rearrange("p i c -> p (i c)"), bank[:, 0 : len(mts) * (b - a)])
-            nc.sync.dma_start(out_rows[:, mts[0] : mts[-1] + 1, a:b], staged[:])
+                nc.tensor.matmul_mx(
+                    bank[:, i * width : (i + 1) * width],
+                    lhsT=w2_codes[:, mt * P : (mt + 1) * P].bitcast(FP8X4),
+                    lhsT_scale=w2_scale[:, mt * P : (mt + 1) * P],
+                    rhs=z_codes[c][:].bitcast(FP8X4),
+                    rhs_scale=z_scale[c][:],
+                    start=True,
+                    stop=True,
+                )
+            copy(dest, bank[:, 0 : len(mts) * width])
+
+        def first_columns(half):
+            staged = keep.tile([P, 2, 128], F32, name=f"early{half}")
+            second(0, (2 * half, 2 * half + 1), staged[:].rearrange("p i c -> p (i c)"), nc.scalar.copy)
+            nc.sync.dma_start(out_rows[:, 2 * half : 2 * half + 2, 0:128], staged[:])
 
         group_z(nc.vector.tensor_copy, 1, 0)
-        group_z(nc.scalar.copy, 1, 1)
         group_z(nc.scalar.copy, 1, 2)
+        group_z(nc.scalar.copy, 1, 1)
         quantize_w2(0)
         quantize_z(0)
-        second((0,), (0, 1), nc.scalar.copy)
+        first_columns(0)
         quantize_w2(1)
-        second((0,), (2, 3), nc.scalar.copy)
-        quantize_z(1)
+        first_columns(1)
         quantize_z(2)
-        second((1,), (0, 1), nc.scalar.copy)
-        second((1,), (2, 3), nc.vector.tensor_copy)
+        quantize_z(1)
         for mt in range(4):
-            second((2,), (mt,), nc.vector.tensor_copy if mt % 2 else nc.scalar.copy)
+            staged = keep.tile([P, 384], F32, name=f"late{mt}")
+            second(2, (mt,), staged[:, 128:384], nc.vector.tensor_copy)
+            if mt == 3:
+                nc.sync.dma_start(out_rows[:, mt, 256:512], staged[:, 128:384])
+            second(1, (mt,), staged[:, 0:128], nc.scalar.copy)
+            if mt == 3:
+                nc.sync.dma_start(out_rows[:, mt, 128:256], staged[:, 0:128])
+            else:
+                nc.sync.dma_start(out_rows[:, mt, 128:512], staged[:])

@@ -29,57 +29,71 @@ def tile_picked_modtrue_gelu_p_kernel(tc, x_words, x_scales, w1, wt, w2, offs, t
     with ExitStack() as ctx:
         lists = ctx.enter_context(tc.tile_pool(name="lists", bufs=1))
         keep = ctx.enter_context(tc.tile_pool(name="keep", bufs=1))
+        held = ctx.enter_context(tc.tile_pool(name="held", bufs=1))
         psum = ctx.enter_context(tc.psum_pool(name="psum", bufs=8))
 
         offs_sb = lists.tile([P, S // 16], U16, name="offs_sb")
         take_sb = lists.tile([P, V // 16], U16, name="take_sb")
 
-        scale_table = keep.tile([P, T], U8, name="scale_table", tag="table_then_w1", align_bytes=64)
+        scale_table = held.tile([P, T], U8, name="scale_table", offset=2048, align_bytes=64)
         for a, b in ((0, 16), (32, 64), (64, P)):
             nc.vector.memset(scale_table[a:b, :].bitcast(I32), 0)
         x_scale = keep.tile([P, S], U8, name="x_scale", align_bytes=64)
         nc.vector.memset(x_scale[:].bitcast(I32), 0)
         nc.sync.dma_start(scale_table[16:32, :].bitcast(I32), x_scales[0].bitcast(I32))
         nc.sync.dma_start(offs_sb[:], offs)
-        w1_raw = keep.tile([P, PACK, H], F32, name="w1_raw", tag="w_raw")
-        nc.sync.dma_start(w1_raw[:], w1.rearrange("(p j) c -> p j c", j=PACK))
-        word_table = keep.tile([P, T], U32, name="word_table", tag="words_then_w1", align_bytes=64)
+        word_table = keep.tile([P, T], U32, name="word_table", tag="words_then_w2", align_bytes=64)
         nc.sync.dma_start(word_table[:].bitcast(I32), x_words[0].rearrange("p n r -> p (n r)").bitcast(I32))
+        w1_rows = w1.rearrange("(p j) c -> p j c", j=PACK)
+        w1_early = keep.tile([P, 3, H], F32, name="w1_early")
+        nc.sync.dma_start(w1_early[:], w1_rows[:, 0:3, :])
         nc.sync.dma_start(take_sb[:], take)
 
-        picked_scale = keep.tile([P, S], U8, name="picked_scale", tag="scale_wt_w2", align_bytes=64)
+        picked_scale = keep.tile([P, S], U8, name="picked_scale", align_bytes=64)
         nc.vector.tensor_copy(picked_scale[:], scale_table[:].indirect(offs_sb[:]))
         for q in range(4):
             nc.sync.dma_start(x_scale[32 * q : 32 * q + 4, :].bitcast(I32), picked_scale[16 + 4 * q : 20 + 4 * q, :].bitcast(I32))
-
-        w1_grouped = {
-            1: keep.tile([P, 2, P, PACK], BF16, name="w1_grouped_odd", tag="table_then_w1", align_bytes=64),
-            0: keep.tile([P, 2, P, PACK], BF16, name="w1_grouped_even", align_bytes=64),
-        }
-        for e in (1, 0):
-            nc.vector.tensor_copy(
-                w1_grouped[e][:].rearrange("p u m j -> p m u j"),
-                w1_raw[:].rearrange("p j (m u e) -> p e m u j", u=2, e=2)[:, e],
-            )
-        w2_raw = keep.tile([P, PACK, N], F32, name="w2_raw", tag="w_raw")
-        nc.sync.dma_start(w2_raw[:], w2.rearrange("(p j) c -> p j c", j=PACK))
-        wt_sb = keep.tile([P, V], F32, name="wt_sb", tag="scale_wt_w2", align_bytes=64)
+        w1_late = held.tile([P, H], F32, name="w1_late", offset=64, align_bytes=64)
+        nc.sync.dma_start(w1_late[:], w1_rows[:, 3, :])
+        wt_sb = held.tile([P, V], F32, name="wt_sb", offset=4096 - 64, align_bytes=64)
         nc.sync.dma_start(wt_sb[:], wt.rearrange("(p j) v -> p j v", j=PACK)[:, 0, :])
-        w1_codes, w1_scale = {}, {}
 
-        def quantize_w1(e, tag):
-            w1_codes[e] = keep.tile([P, H // 2], U32, name=f"w1_codes{e}", tag=tag, align_bytes=64)
-            w1_scale[e] = keep.tile([P, H // 2], U8, name=f"w1_scale{e}", align_bytes=64)
-            nc.vector.quantize_mx(w1_codes[e][:].bitcast(FP8X4), w1_scale[e][:], w1_grouped[e][:].rearrange("p u m j -> p (u m j)"))
+        x_codes = keep.tile([P, S], U32, name="x_codes", align_bytes=64)
+        nc.vector.tensor_copy(x_codes[:], word_table[:].indirect(offs_sb[:]))
+        w2_raw = keep.tile([P, PACK, N], F32, name="w2_raw", tag="words_then_w2", align_bytes=64)
+        nc.sync.dma_start(w2_raw[:], w2.rearrange("(p j) c -> p j c", j=PACK))
 
-        quantize_w1(1, "w1_codes_odd")
+        w1_grouped = {}
+        w1_codes = {e: keep.tile([P, H // 2], U32, name=f"w1_codes{e}", align_bytes=64) for e in (1, 0)}
+        w1_scale = {e: keep.tile([P, H // 2], U8, name=f"w1_scale{e}", align_bytes=64) for e in (1, 0)}
 
-        x_codes = keep.tile([P, S], U32, name="x_codes", tag="table_then_w1", align_bytes=64)
-        for h in range(2):
+        def group_early(e):
+            w1_grouped[e] = keep.tile([P, 2, P, PACK], BF16, name=f"w1_grouped{e}", tag="w1_grouped", align_bytes=64)
             nc.vector.tensor_copy(
-                x_codes[:, h * HALF : (h + 1) * HALF], word_table[:].indirect(offs_sb[:, h * HALF // 16 : (h + 1) * HALF // 16])
+                w1_grouped[e][:, :, :, 0:3].rearrange("p u m j -> p m u j"),
+                w1_early[:].rearrange("p j (m u e) -> p e m u j", u=2, e=2)[:, e],
             )
-        quantize_w1(0, "words_then_w1")
+
+        def group_late(e, u0, u1):
+            nc.vector.tensor_copy(
+                w1_grouped[e][:, u0:u1, :, 3],
+                w1_late[:].rearrange("p (m u e) -> p e u m", u=2, e=2)[:, e, u0:u1],
+            )
+
+        def quantize_w1(e, u0, u1):
+            cols = slice(u0 * P, u1 * P)
+            nc.vector.quantize_mx(
+                w1_codes[e][:, cols].bitcast(FP8X4), w1_scale[e][:, cols], w1_grouped[e][:, u0:u1].rearrange("p u m j -> p (u m j)")
+            )
+
+        group_early(1)
+        group_late(1, 0, 1)
+        group_late(1, 1, 2)
+        quantize_w1(1, 0, 1)
+        quantize_w1(1, 1, 2)
+        group_early(0)
+        group_late(0, 0, 2)
+        quantize_w1(0, 0, 2)
 
         def first(t, dest, cols):
             at = (t // 2) * P
@@ -100,17 +114,10 @@ def tile_picked_modtrue_gelu_p_kernel(tc, x_words, x_scales, w1, wt, w2, offs, t
             y[t] = [(psum.tile([P, S], F32, name="bank")[:], slice(0, S))]
         for h in range(2):
             first(ORDER[0], y[ORDER[0]][h][0], halves[h])
-            first(ORDER[1], y[ORDER[1]][0][0][:, halves[h]], halves[h])
-        for t in ORDER[2:]:
+        for t in ORDER[1:]:
             first(t, y[t][0][0], slice(0, S))
 
         picked = {}
-
-        def pick(t):
-            act = keep.tile([P, S], F32, name=f"act{t}")
-            nc.scalar.activation(act[:], y[t][0][0], GELU)
-            picked[t] = keep.tile([P, V], F32, name=f"picked{t}")
-            nc.vector.tensor_copy(picked[t][:], act[:].indirect(take_sb[:]))
 
         pairs = [keep.tile([P, 2, S], F32, name=f"pair{u}") for u in range(2)]
         window = {}
@@ -120,8 +127,8 @@ def tile_picked_modtrue_gelu_p_kernel(tc, x_words, x_scales, w1, wt, w2, offs, t
 
         w2_grouped = keep.tile([P, N, PACK], BF16, name="w2_grouped", align_bytes=64)
 
-        def group_w2(mt):
-            cols = slice(mt * P, (mt + 1) * P)
+        def group_w2(a, b):
+            cols = slice(a, b)
             nc.scalar.copy(
                 w2_grouped[:, cols, :].rearrange("p (c i) j -> p c j i", i=4),
                 w2_raw[:, :, cols].rearrange("p j (c i) -> p c j i", i=4),
@@ -132,35 +139,51 @@ def tile_picked_modtrue_gelu_p_kernel(tc, x_words, x_scales, w1, wt, w2, offs, t
 
         z_grouped = [keep.tile([P, b - a, PACK], BF16, name=f"z_grouped{a}", align_bytes=64) for a, b in CHUNKS]
 
-        def group_z(copy, u, c):
+        def group_z(copy, u, c, lo=None, hi=None):
             a, b = CHUNKS[c]
-            copy(z_grouped[c][:, :, 2 * u : 2 * u + 2], pairs[u][:, :, a:b].rearrange("p s c -> p c s"))
+            lo, hi = (a, b) if lo is None else (lo, hi)
+            copy(z_grouped[c][:, lo - a : hi - a, 2 * u : 2 * u + 2], pairs[u][:, :, lo:hi].rearrange("p s c -> p c s"))
 
+        def fetch(t, source):
+            got = keep.tile([P, V], F32, name=f"got{t}")
+            nc.vector.tensor_copy(got[:], source.indirect(take_sb[:]))
+            return got
+
+        def activate(t, raw):
+            picked[t] = keep.tile([P, V], F32, name=f"picked{t}")
+            nc.scalar.activation(picked[t][:], raw[:], GELU)
+
+        act = keep.tile([P, S], F32, name="act")
         for part, cols in y[1]:
-            nc.vector.tensor_copy(window[1][:, cols], part)
-        raw = keep.tile([P, V], F32, name="raw")
-        nc.vector.tensor_copy(raw[:], window[1].indirect(take_sb[:]))
-        pick(3)
-        pick(0)
-        picked[1] = keep.tile([P, V], F32, name="picked1")
-        nc.scalar.activation(picked[1][:], raw[:], GELU)
+            nc.scalar.activation(act[:, cols], part, GELU)
+        picked[1] = fetch(1, act[:])
+        nc.scalar.copy(window[3], y[3][0][0])
+        raw3 = fetch(3, window[3])
+        for part, cols in y[1]:
+            nc.scalar.copy(window[1][:, cols], part)
         scatter(1)
-        pick(2)
-        for t in (3, 0, 2):
-            nc.scalar.copy(window[t][:, 0:S], y[t][0][0])
+        nc.scalar.copy(window[0][:, 0:S], y[0][0][0])
+        raw0 = fetch(0, window[0])
+        activate(3, raw3)
         scatter(3)
-        group_w2(0)
+        nc.scalar.copy(window[2][:, 0:S], y[2][0][0])
+        raw2 = fetch(2, window[2])
+        group_w2(0, 128)
+        group_w2(128, 256)
+        activate(0, raw0)
         nc.scalar.copy(pairs[0][:, 1, :], window[1])
         scatter(0)
-        group_w2(1)
-        group_w2(2)
+        group_w2(256, 384)
+        group_w2(384, 496)
+        activate(2, raw2)
         nc.scalar.copy(pairs[1][:, 1, :], window[3])
         scatter(2)
-        group_w2(3)
-        for c in (0, 2, 1):
-            group_z(nc.scalar.copy, 0, c)
+        group_z(nc.scalar.copy, 0, 0)
+        group_z(nc.scalar.copy, 0, 1)
+        group_w2(496, 512)
+        group_z(nc.scalar.copy, 0, 2)
 
-        w2_codes = keep.tile([P, N], U32, name="w2_codes", tag="scale_wt_w2", align_bytes=64)
+        w2_codes = held.tile([P, N], U32, name="w2_codes", offset=4096, align_bytes=64)
         w2_scale = keep.tile([P, N], U8, name="w2_scale", align_bytes=64)
 
         def quantize_w2(half):
@@ -169,51 +192,61 @@ def tile_picked_modtrue_gelu_p_kernel(tc, x_words, x_scales, w1, wt, w2, offs, t
                 w2_codes[:, cols].bitcast(FP8X4), w2_scale[:, cols], w2_grouped[:, cols, :].rearrange("p c j -> p (c j)")
             )
 
-        z_codes = [keep.tile([P, b - a], U32, name=f"z_codes{a}", align_bytes=64) for a, b in CHUNKS]
-        z_scale = [keep.tile([P, b - a], U8, name=f"z_scale{a}", align_bytes=64) for a, b in CHUNKS]
+        z_codes = keep.tile([P, S], U32, name="z_codes", align_bytes=64)
+        z_scale = keep.tile([P, S], U8, name="z_scale", align_bytes=64)
 
         def quantize_z(c):
-            nc.vector.quantize_mx(z_codes[c][:].bitcast(FP8X4), z_scale[c][:], z_grouped[c][:].rearrange("p c j -> p (c j)"))
+            a, b = CHUNKS[c]
+            nc.vector.quantize_mx(z_codes[:, a:b].bitcast(FP8X4), z_scale[:, a:b], z_grouped[c][:].rearrange("p c j -> p (c j)"))
 
         out_rows = out.rearrange("(mt p) j -> p mt j", p=P)
 
-        def second(c, mts, dest, copy):
-            width = CHUNKS[c][1] - CHUNKS[c][0]
-            bank = psum.tile([P, S], F32, name="bank")
-            for i, mt in enumerate(mts):
-                nc.tensor.matmul_mx(
-                    bank[:, i * width : (i + 1) * width],
-                    lhsT=w2_codes[:, mt * P : (mt + 1) * P].bitcast(FP8X4),
-                    lhsT_scale=w2_scale[:, mt * P : (mt + 1) * P],
-                    rhs=z_codes[c][:].bitcast(FP8X4),
-                    rhs_scale=z_scale[c][:],
-                    start=True,
-                    stop=True,
-                )
-            copy(dest, bank[:, 0 : len(mts) * width])
+        def second(mt, a, b, dest):
+            nc.tensor.matmul_mx(
+                dest,
+                lhsT=w2_codes[:, mt * P : (mt + 1) * P].bitcast(FP8X4),
+                lhsT_scale=w2_scale[:, mt * P : (mt + 1) * P],
+                rhs=z_codes[:, a:b].bitcast(FP8X4),
+                rhs_scale=z_scale[:, a:b],
+                start=True,
+                stop=True,
+            )
 
-        def first_columns(half):
-            staged = keep.tile([P, 2, 128], F32, name=f"early{half}")
-            second(0, (2 * half, 2 * half + 1), staged[:].rearrange("p i c -> p (i c)"), nc.scalar.copy)
-            nc.sync.dma_start(out_rows[:, 2 * half : 2 * half + 2, 0:128], staged[:])
+        def new_bank():
+            return psum.tile([P, S], F32, name="bank")
 
-        group_z(nc.vector.tensor_copy, 1, 0)
-        group_z(nc.scalar.copy, 1, 2)
-        group_z(nc.scalar.copy, 1, 1)
+        def narrow(c, mt, copy):
+            a, b = CHUNKS[c]
+            bank = new_bank()
+            for i in range(2):
+                second(mt + i, a, b, bank[:, i * P : (i + 1) * P])
+            staged = keep.tile([P, 2, P], F32, name=f"narrow{c}_{mt}")
+            copy(staged[:].rearrange("p i c -> p (i c)"), bank[:, 0 : 2 * P])
+            nc.sync.dma_start(out_rows[:, mt : mt + 2, a:b], staged[:])
+
+        by_vector, by_scalar = nc.vector.tensor_copy, nc.scalar.copy
+        group_z(by_vector, 1, 0)
+        group_z(by_scalar, 1, 1)
+        group_z(by_scalar, 1, 2, 256, 384)
         quantize_w2(0)
         quantize_z(0)
-        first_columns(0)
         quantize_w2(1)
-        first_columns(1)
-        quantize_z(2)
         quantize_z(1)
-        for mt in range(4):
-            staged = keep.tile([P, 384], F32, name=f"late{mt}")
-            second(2, (mt,), staged[:, 128:384], nc.vector.tensor_copy)
-            if mt == 3:
-                nc.sync.dma_start(out_rows[:, mt, 256:512], staged[:, 128:384])
-            second(1, (mt,), staged[:, 0:128], nc.scalar.copy)
-            if mt == 3:
-                nc.sync.dma_start(out_rows[:, mt, 128:256], staged[:, 0:128])
-            else:
-                nc.sync.dma_start(out_rows[:, mt, 128:512], staged[:])
+        group_z(by_vector, 1, 2, 384, 512)
+        quantize_z(2)
+        narrow(0, 0, by_scalar)
+        narrow(0, 2, by_scalar)
+        narrow(1, 0, by_vector)
+        narrow(1, 2, by_scalar)
+        for mt, copy in ((0, by_vector), (1, by_scalar), (2, by_vector)):
+            bank = new_bank()
+            second(mt, 256, 512, bank[:, 0:256])
+            staged = keep.tile([P, HALF], F32, name=f"wide{mt}")
+            copy(staged[:], bank[:, 0:256])
+            nc.sync.dma_start(out_rows[:, mt, 256:512], staged[:])
+        staged = keep.tile([P, HALF], F32, name="wide3")
+        for i, copy in enumerate((by_scalar, by_vector)):
+            bank = new_bank()
+            second(3, 256 + i * P, 384 + i * P, bank[:, 0:P])
+            copy(staged[:, i * P : (i + 1) * P], bank[:, 0:P])
+        nc.sync.dma_start(out_rows[:, 3, 256:512], staged[:])

@@ -180,7 +180,6 @@ def tile_picked_modtrue_gelu_p_kernel(tc, x_words, x_scales, w1, wt, w2, offs, t
         scatter(2)
         group_z(nc.scalar.copy, 0, 0)
         group_z(nc.scalar.copy, 0, 1)
-        group_w2(496, 512)
         group_z(nc.scalar.copy, 0, 2)
 
         w2_codes = held.tile([P, N], U32, name="w2_codes", offset=4096, align_bytes=64)
@@ -215,35 +214,31 @@ def tile_picked_modtrue_gelu_p_kernel(tc, x_words, x_scales, w1, wt, w2, offs, t
         def new_bank():
             return psum.tile([P, S], F32, name="bank")
 
-        def narrow(c, mt, copy):
-            a, b = CHUNKS[c]
+        def store(mt, a, cuts, copy):
             bank = new_bank()
-            for i in range(2):
-                second(mt + i, a, b, bank[:, i * P : (i + 1) * P])
-            staged = keep.tile([P, 2, P], F32, name=f"narrow{c}_{mt}")
-            copy(staged[:].rearrange("p i c -> p (i c)"), bank[:, 0 : 2 * P])
-            nc.sync.dma_start(out_rows[:, mt : mt + 2, a:b], staged[:])
+            for lo, hi in zip(cuts, cuts[1:]):
+                second(mt, lo, hi, bank[:, lo - a : hi - a])
+            staged = keep.tile([P, HALF], F32, name=f"staged{mt}_{a}")
+            copy(staged[:], bank[:, 0:HALF])
+            nc.sync.dma_start(out_rows[:, mt, a : a + HALF], staged[:])
 
         by_vector, by_scalar = nc.vector.tensor_copy, nc.scalar.copy
         group_z(by_vector, 1, 0)
         group_z(by_scalar, 1, 1)
-        group_z(by_scalar, 1, 2, 256, 384)
+        group_w2(496, 512)
+        group_z(by_scalar, 1, 2)
         quantize_w2(0)
         quantize_z(0)
-        quantize_w2(1)
         quantize_z(1)
-        group_z(by_vector, 1, 2, 384, 512)
+        quantize_w2(1)
         quantize_z(2)
-        narrow(0, 0, by_scalar)
-        narrow(0, 2, by_scalar)
-        narrow(1, 0, by_vector)
-        narrow(1, 2, by_scalar)
-        for mt, copy in ((0, by_vector), (1, by_scalar), (2, by_vector)):
-            bank = new_bank()
-            second(mt, 256, 512, bank[:, 0:256])
-            staged = keep.tile([P, HALF], F32, name=f"wide{mt}")
-            copy(staged[:], bank[:, 0:256])
-            nc.sync.dma_start(out_rows[:, mt, 256:512], staged[:])
+        store(0, 0, (0, 128, 256), by_scalar)
+        store(1, 0, (0, 256), by_scalar)
+        store(2, 0, (0, 256), by_vector)
+        store(3, 0, (0, 256), by_scalar)
+        store(0, 256, (256, 512), by_vector)
+        store(1, 256, (256, 512), by_scalar)
+        store(2, 256, (256, 512), by_vector)
         staged = keep.tile([P, HALF], F32, name="wide3")
         for i, copy in enumerate((by_scalar, by_vector)):
             bank = new_bank()

@@ -20,7 +20,6 @@ MULT = mybir.AluOpType.mult
 P = 128
 PACK = 4
 HALF = S // 2
-ORDER = (1, 3, 0, 2)
 CHUNKS = ((0, 128), (128, 256), (256, 512))
 
 
@@ -45,16 +44,15 @@ def tile_picked_modtrue_gelu_p_kernel(tc, x_words, x_scales, w1, wt, w2, offs, t
         word_table = keep.tile([P, T], U32, name="word_table", tag="words_then_w2", align_bytes=64)
         nc.sync.dma_start(word_table[:].bitcast(I32), x_words[0].rearrange("p n r -> p (n r)").bitcast(I32))
         w1_rows = w1.rearrange("(p j) c -> p j c", j=PACK)
-        w1_early = keep.tile([P, 3, H], F32, name="w1_early")
-        nc.sync.dma_start(w1_early[:], w1_rows[:, 0:3, :])
+        w1_raw = keep.tile([P, PACK, H], F32, name="w1_raw")
+        for a, b in ((0, 2), (2, 3), (3, 4)):
+            nc.sync.dma_start(w1_raw[:, a:b, :], w1_rows[:, a:b, :])
         nc.sync.dma_start(take_sb[:], take)
 
         picked_scale = keep.tile([P, S], U8, name="picked_scale", align_bytes=64)
         nc.vector.tensor_copy(picked_scale[:], scale_table[:].indirect(offs_sb[:]))
         for q in range(4):
             nc.sync.dma_start(x_scale[32 * q : 32 * q + 4, :].bitcast(I32), picked_scale[16 + 4 * q : 20 + 4 * q, :].bitcast(I32))
-        w1_late = held.tile([P, H], F32, name="w1_late", offset=64, align_bytes=64)
-        nc.sync.dma_start(w1_late[:], w1_rows[:, 3, :])
         wt_sb = held.tile([P, V], F32, name="wt_sb", offset=4096 - 64, align_bytes=64)
         nc.sync.dma_start(wt_sb[:], wt.rearrange("(p j) v -> p j v", j=PACK)[:, 0, :])
 
@@ -67,17 +65,17 @@ def tile_picked_modtrue_gelu_p_kernel(tc, x_words, x_scales, w1, wt, w2, offs, t
         w1_codes = {e: keep.tile([P, H // 2], U32, name=f"w1_codes{e}", align_bytes=64) for e in (1, 0)}
         w1_scale = {e: keep.tile([P, H // 2], U8, name=f"w1_scale{e}", align_bytes=64) for e in (1, 0)}
 
-        def group_early(e):
+        def group_rows(e, rows):
             w1_grouped[e] = keep.tile([P, 2, P, PACK], BF16, name=f"w1_grouped{e}", tag="w1_grouped", align_bytes=64)
             nc.vector.tensor_copy(
-                w1_grouped[e][:, :, :, 0:3].rearrange("p u m j -> p m u j"),
-                w1_early[:].rearrange("p j (m u e) -> p e m u j", u=2, e=2)[:, e],
+                w1_grouped[e][:, :, :, 0:rows].rearrange("p u m j -> p m u j"),
+                w1_raw[:, 0:rows, :].rearrange("p j (m u e) -> p e m u j", u=2, e=2)[:, e],
             )
 
-        def group_late(e, u0, u1):
+        def group_late(e, u):
             nc.vector.tensor_copy(
-                w1_grouped[e][:, u0:u1, :, 3],
-                w1_late[:].rearrange("p (m u e) -> p e u m", u=2, e=2)[:, e, u0:u1],
+                w1_grouped[e][:, u, :, 3],
+                w1_raw[:, 3, :].rearrange("p (m u e) -> p e u m", u=2, e=2)[:, e, u],
             )
 
         def quantize_w1(e, u0, u1):
@@ -86,14 +84,27 @@ def tile_picked_modtrue_gelu_p_kernel(tc, x_words, x_scales, w1, wt, w2, offs, t
                 w1_codes[e][:, cols].bitcast(FP8X4), w1_scale[e][:, cols], w1_grouped[e][:, u0:u1].rearrange("p u m j -> p (u m j)")
             )
 
-        group_early(1)
-        group_late(1, 0, 1)
-        group_late(1, 1, 2)
+        group_rows(1, 2)
+        nc.vector.tensor_copy(
+            w1_grouped[1][:, :, :, 2].rearrange("p u m -> p m u"),
+            w1_raw[:, 2, :].rearrange("p (m u e) -> p e m u", u=2, e=2)[:, 1],
+        )
+        group_late(1, 0)
+        group_late(1, 1)
         quantize_w1(1, 0, 1)
         quantize_w1(1, 1, 2)
-        group_early(0)
-        group_late(0, 0, 2)
-        quantize_w1(0, 0, 2)
+        even = keep.tile([P, 2, P, PACK], BF16, name="w1_grouped0", tag="w1_grouped", align_bytes=64)
+        for m in (slice(0, 64), slice(64, P)):
+            nc.vector.tensor_copy(
+                even[:, :, m, :].rearrange("p u m j -> p m u j"),
+                w1_raw[:].rearrange("p j (m u e) -> p e m u j", u=2, e=2)[:, 0, m],
+            )
+        for at in (0, 64):
+            for u in range(2):
+                cols = slice(u * P + at, u * P + at + 64)
+                nc.vector.quantize_mx(
+                    w1_codes[0][:, cols].bitcast(FP8X4), w1_scale[0][:, cols], even[:, u, at : at + 64, :].rearrange("p m j -> p (m j)")
+                )
 
         def first(t, dest, cols):
             at = (t // 2) * P
@@ -107,15 +118,15 @@ def tile_picked_modtrue_gelu_p_kernel(tc, x_words, x_scales, w1, wt, w2, offs, t
                 stop=True,
             )
 
-        halves = [slice(h * HALF, (h + 1) * HALF) for h in range(2)]
-        y = {}
-        y[ORDER[0]] = [(psum.tile([P, S], F32, name="bank")[:, 0:HALF], cols) for cols in halves]
-        for t in ORDER[1:]:
-            y[t] = [(psum.tile([P, S], F32, name="bank")[:], slice(0, S))]
-        for h in range(2):
-            first(ORDER[0], y[ORDER[0]][h][0], halves[h])
-        for t in ORDER[1:]:
-            first(t, y[t][0][0], slice(0, S))
+        def product(t, a, b):
+            bank = psum.tile([P, S], F32, name="bank")[:, 0 : b - a]
+            first(t, bank, slice(a, b))
+            return bank, slice(a, b)
+
+        y1 = [product(1, a, b) for a, b in ((0, 128), (128, 256), (256, 384), (384, 512))]
+        y3 = [product(3, a, b) for a, b in ((0, 256), (256, 512))]
+        y0 = product(0, 0, S)
+        y2 = product(2, 0, S)
 
         picked = {}
 
@@ -154,19 +165,20 @@ def tile_picked_modtrue_gelu_p_kernel(tc, x_words, x_scales, w1, wt, w2, offs, t
             nc.scalar.activation(picked[t][:], raw[:], GELU)
 
         act = keep.tile([P, S], F32, name="act")
-        for part, cols in y[1]:
+        for part, cols in y1:
             nc.scalar.activation(act[:, cols], part, GELU)
         picked[1] = fetch(1, act[:])
-        nc.scalar.copy(window[3], y[3][0][0])
+        for part, cols in y3:
+            nc.scalar.copy(window[3][:, cols], part)
         raw3 = fetch(3, window[3])
-        for part, cols in y[1]:
+        for part, cols in y1:
             nc.scalar.copy(window[1][:, cols], part)
         scatter(1)
-        nc.scalar.copy(window[0][:, 0:S], y[0][0][0])
+        nc.scalar.copy(window[0][:, 0:S], y0[0])
         raw0 = fetch(0, window[0])
         activate(3, raw3)
         scatter(3)
-        nc.scalar.copy(window[2][:, 0:S], y[2][0][0])
+        nc.scalar.copy(window[2][:, 0:S], y2[0])
         raw2 = fetch(2, window[2])
         group_w2(0, 128)
         group_w2(128, 256)

@@ -52,7 +52,7 @@ def tile_picked_modtrue_gelu_p_kernel(tc, x_words, x_scales, w1, wt, w2, offs, t
         picked_scale = keep.tile([P, S], U8, name="picked_scale", align_bytes=64)
         nc.vector.tensor_copy(picked_scale[:], scale_table[:].indirect(offs_sb[:]))
         for q in range(4):
-            nc.sync.dma_start(x_scale[32 * q : 32 * q + 4, :].bitcast(I32), picked_scale[16 + 4 * q : 20 + 4 * q, :].bitcast(I32))
+            nc.scalar.dma_start(x_scale[32 * q : 32 * q + 4, :].bitcast(I32), picked_scale[16 + 4 * q : 20 + 4 * q, :].bitcast(I32))
         wt_sb = held.tile([P, V], F32, name="wt_sb", offset=4096 - 64, align_bytes=64)
         nc.sync.dma_start(wt_sb[:], wt.rearrange("(p j) v -> p j v", j=PACK)[:, 0, :])
 

@@ -20,27 +20,31 @@ MULT = mybir.AluOpType.mult
 P = 128
 PACK = 4
 HALF = S // 2
-CHUNKS = ((0, 128), (128, 256), (256, 512))
+BANKS = 8
+RANGES = ((0, P), (P, HALF), (HALF, S))
+W2_LATE = 16
 
 
 def tile_picked_modtrue_gelu_p_kernel(tc, x_words, x_scales, w1, wt, w2, offs, take, out):
     nc = tc.nc
+    by_vector, by_scalar = nc.vector.tensor_copy, nc.scalar.copy
     with ExitStack() as ctx:
         lists = ctx.enter_context(tc.tile_pool(name="lists", bufs=1))
         keep = ctx.enter_context(tc.tile_pool(name="keep", bufs=1))
-        held = ctx.enter_context(tc.tile_pool(name="held", bufs=1))
-        psum = ctx.enter_context(tc.psum_pool(name="psum", bufs=8))
+        psum = ctx.enter_context(tc.psum_pool(name="psum", bufs=BANKS))
+
 
         offs_sb = lists.tile([P, S // 16], U16, name="offs_sb")
         take_sb = lists.tile([P, V // 16], U16, name="take_sb")
 
-        scale_table = held.tile([P, T], U8, name="scale_table", offset=2048, align_bytes=64)
+        scale_table = keep.tile([P, T], U8, name="scale_table", tag="scales_wt_w2", align_bytes=64)
         for a, b in ((0, 16), (32, 64), (64, P)):
             nc.vector.memset(scale_table[a:b, :].bitcast(I32), 0)
         x_scale = keep.tile([P, S], U8, name="x_scale", align_bytes=64)
         nc.vector.memset(x_scale[:].bitcast(I32), 0)
-        nc.sync.dma_start(scale_table[16:32, :].bitcast(I32), x_scales[0].bitcast(I32))
+        nc.scalar.dma_start(scale_table[16:32, :].bitcast(I32), x_scales[0].bitcast(I32))
         nc.sync.dma_start(offs_sb[:], offs)
+
         word_table = keep.tile([P, T], U32, name="word_table", tag="words_then_w2", align_bytes=64)
         nc.sync.dma_start(word_table[:].bitcast(I32), x_words[0].rearrange("p n r -> p (n r)").bitcast(I32))
         w1_rows = w1.rearrange("(p j) c -> p j c", j=PACK)
@@ -50,169 +54,153 @@ def tile_picked_modtrue_gelu_p_kernel(tc, x_words, x_scales, w1, wt, w2, offs, t
         nc.sync.dma_start(take_sb[:], take)
 
         picked_scale = keep.tile([P, S], U8, name="picked_scale", align_bytes=64)
-        nc.vector.tensor_copy(picked_scale[:], scale_table[:].indirect(offs_sb[:]))
+        by_vector(picked_scale[:], scale_table[:].indirect(offs_sb[:]))
         for q in range(4):
             nc.scalar.dma_start(x_scale[32 * q : 32 * q + 4, :].bitcast(I32), picked_scale[16 + 4 * q : 20 + 4 * q, :].bitcast(I32))
-        wt_sb = held.tile([P, V], F32, name="wt_sb", offset=4096 - 64, align_bytes=64)
+        wt_sb = keep.tile([P, V], F32, name="wt_sb", tag="scales_wt_w2", align_bytes=64)
         nc.sync.dma_start(wt_sb[:], wt.rearrange("(p j) v -> p j v", j=PACK)[:, 0, :])
 
         x_codes = keep.tile([P, S], U32, name="x_codes", align_bytes=64)
-        nc.vector.tensor_copy(x_codes[:], word_table[:].indirect(offs_sb[:]))
+        by_vector(x_codes[:], word_table[:].indirect(offs_sb[:]))
         w2_raw = keep.tile([P, PACK, N], F32, name="w2_raw", tag="words_then_w2", align_bytes=64)
         nc.sync.dma_start(w2_raw[:], w2.rearrange("(p j) c -> p j c", j=PACK))
 
-        w1_grouped = {}
+        w1_cols = w1_raw[:].rearrange("p j (m u e) -> p e m u j", u=2, e=2)
         w1_codes = {e: keep.tile([P, H // 2], U32, name=f"w1_codes{e}", align_bytes=64) for e in (1, 0)}
         w1_scale = {e: keep.tile([P, H // 2], U8, name=f"w1_scale{e}", align_bytes=64) for e in (1, 0)}
 
-        def group_rows(e, rows):
-            w1_grouped[e] = keep.tile([P, 2, P, PACK], BF16, name=f"w1_grouped{e}", tag="w1_grouped", align_bytes=64)
-            nc.vector.tensor_copy(
-                w1_grouped[e][:, :, :, 0:rows].rearrange("p u m j -> p m u j"),
-                w1_raw[:, 0:rows, :].rearrange("p j (m u e) -> p e m u j", u=2, e=2)[:, e],
-            )
-
-        def group_late(e, u):
-            nc.vector.tensor_copy(
-                w1_grouped[e][:, u, :, 3],
-                w1_raw[:, 3, :].rearrange("p (m u e) -> p e u m", u=2, e=2)[:, e, u],
-            )
-
-        def quantize_w1(e, u0, u1):
-            cols = slice(u0 * P, u1 * P)
+        def quantize_w1(e, grouped, u, a, b):
+            cols = slice(u * P + a, u * P + b)
             nc.vector.quantize_mx(
-                w1_codes[e][:, cols].bitcast(FP8X4), w1_scale[e][:, cols], w1_grouped[e][:, u0:u1].rearrange("p u m j -> p (u m j)")
+                w1_codes[e][:, cols].bitcast(FP8X4), w1_scale[e][:, cols], grouped[:, u, a:b, :].rearrange("p m j -> p (m j)")
             )
 
-        group_rows(1, 2)
-        nc.vector.tensor_copy(
-            w1_grouped[1][:, :, :, 2].rearrange("p u m -> p m u"),
-            w1_raw[:, 2, :].rearrange("p (m u e) -> p e m u", u=2, e=2)[:, 1],
-        )
-        group_late(1, 0)
-        group_late(1, 1)
-        quantize_w1(1, 0, 1)
-        quantize_w1(1, 1, 2)
-        even = keep.tile([P, 2, P, PACK], BF16, name="w1_grouped0", tag="w1_grouped", align_bytes=64)
-        for m in (slice(0, 64), slice(64, P)):
-            nc.vector.tensor_copy(
-                even[:, :, m, :].rearrange("p u m j -> p m u j"),
-                w1_raw[:].rearrange("p j (m u e) -> p e m u j", u=2, e=2)[:, 0, m],
-            )
-        for at in (0, 64):
+        odd = keep.tile([P, 2, P, PACK], BF16, name="w1_odd", tag="w1_grouped", align_bytes=64)
+        odd_cols = odd[:].rearrange("p u m j -> p m u j")
+        by_vector(odd_cols[:, :, :, 0:2], w1_cols[:, 1, :, :, 0:2])
+        by_vector(odd_cols[:, :, :, 2], w1_cols[:, 1, :, :, 2])
+        for u in range(2):
+            by_vector(odd_cols[:, :, u, 3], w1_cols[:, 1, :, u, 3])
+        for u in range(2):
+            quantize_w1(1, odd, u, 0, P)
+        even = keep.tile([P, 2, P, PACK], BF16, name="w1_even", tag="w1_grouped", align_bytes=64)
+        column_halves = ((0, P // 2), (P // 2, P))
+        for a, b in column_halves:
+            by_vector(even[:].rearrange("p u m j -> p m u j")[:, a:b], w1_cols[:, 0, a:b])
+        for a, b in column_halves:
             for u in range(2):
-                cols = slice(u * P + at, u * P + at + 64)
-                nc.vector.quantize_mx(
-                    w1_codes[0][:, cols].bitcast(FP8X4), w1_scale[0][:, cols], even[:, u, at : at + 64, :].rearrange("p m j -> p (m j)")
+                quantize_w1(0, even, u, a, b)
+
+        def new_bank():
+            return psum.tile([P, S], F32, name="bank")
+
+        def first_product(t, parts):
+            at, width, made = (t // 2) * P, S // parts, []
+            for a in range(0, S, width):
+                tokens = slice(a, a + width)
+                values = new_bank()[:, 0:width]
+                nc.tensor.matmul_mx(
+                    values,
+                    lhsT=w1_codes[t % 2][:, at : at + P].bitcast(FP8X4),
+                    lhsT_scale=w1_scale[t % 2][:, at : at + P],
+                    rhs=x_codes[:, tokens].bitcast(FP8X4),
+                    rhs_scale=x_scale[:, tokens],
+                    start=True,
+                    stop=True,
                 )
+                made.append((values, tokens))
+            return made
 
-        def first(t, dest, cols):
-            at = (t // 2) * P
-            nc.tensor.matmul_mx(
-                dest,
-                lhsT=w1_codes[t % 2][:, at : at + P].bitcast(FP8X4),
-                lhsT_scale=w1_scale[t % 2][:, at : at + P],
-                rhs=x_codes[:, cols].bitcast(FP8X4),
-                rhs_scale=x_scale[:, cols],
-                start=True,
-                stop=True,
-            )
-
-        def product(t, a, b):
-            bank = psum.tile([P, S], F32, name="bank")[:, 0 : b - a]
-            first(t, bank, slice(a, b))
-            return bank, slice(a, b)
-
-        y1 = [product(1, a, b) for a, b in ((0, 128), (128, 256), (256, 384), (384, 512))]
-        y3 = [product(3, a, b) for a, b in ((0, 256), (256, 512))]
-        y0 = product(0, 0, S)
-        y2 = product(2, 0, S)
-
-        picked = {}
+        y = {t: first_product(t, parts) for t, parts in ((1, 4), (3, 2), (0, 1), (2, 1))}
 
         pairs = [keep.tile([P, 2, S], F32, name=f"pair{u}") for u in range(2)]
         window = {}
         for u in range(2):
             window[2 * u] = pairs[u][:].rearrange("p s c -> p (s c)")
             window[2 * u + 1] = keep.tile([P, S], F32, name=f"single{u}")[:]
-
         w2_grouped = keep.tile([P, N, PACK], BF16, name="w2_grouped", align_bytes=64)
+        z_grouped = [keep.tile([P, b - a, PACK], BF16, name=f"z_grouped{a}", align_bytes=64) for a, b in RANGES]
 
-        def group_w2(a, b):
-            cols = slice(a, b)
-            nc.scalar.copy(
-                w2_grouped[:, cols, :].rearrange("p (c i) j -> p c j i", i=4),
-                w2_raw[:, :, cols].rearrange("p j (c i) -> p c j i", i=4),
-            )
-
-        def scatter(t):
-            nc.vector.tensor_tensor(window[t].indirect(take_sb[:]), picked[t][:], wt_sb[:], MULT)
-
-        z_grouped = [keep.tile([P, b - a, PACK], BF16, name=f"z_grouped{a}", align_bytes=64) for a, b in CHUNKS]
-
-        def group_z(copy, u, c, lo=None, hi=None):
-            a, b = CHUNKS[c]
-            lo, hi = (a, b) if lo is None else (lo, hi)
-            copy(z_grouped[c][:, lo - a : hi - a, 2 * u : 2 * u + 2], pairs[u][:, :, lo:hi].rearrange("p s c -> p c s"))
+        def fill_window(t):
+            for values, tokens in y[t]:
+                by_scalar(window[t][:, tokens], values)
 
         def fetch(t, source):
             got = keep.tile([P, V], F32, name=f"got{t}")
-            nc.vector.tensor_copy(got[:], source.indirect(take_sb[:]))
+            by_vector(got[:], source.indirect(take_sb[:]))
             return got
 
         def activate(t, raw):
-            picked[t] = keep.tile([P, V], F32, name=f"picked{t}")
-            nc.scalar.activation(picked[t][:], raw[:], GELU)
+            done = keep.tile([P, V], F32, name=f"activated{t}")
+            nc.scalar.activation(done[:], raw[:], GELU)
+            return done
 
-        act = keep.tile([P, S], F32, name="act")
-        for part, cols in y1:
-            nc.scalar.activation(act[:, cols], part, GELU)
-        picked[1] = fetch(1, act[:])
-        for part, cols in y3:
-            nc.scalar.copy(window[3][:, cols], part)
-        raw3 = fetch(3, window[3])
-        for part, cols in y1:
-            nc.scalar.copy(window[1][:, cols], part)
-        scatter(1)
-        nc.scalar.copy(window[0][:, 0:S], y0[0])
-        raw0 = fetch(0, window[0])
-        activate(3, raw3)
-        scatter(3)
-        nc.scalar.copy(window[2][:, 0:S], y2[0])
-        raw2 = fetch(2, window[2])
-        group_w2(0, 128)
-        group_w2(128, 256)
-        activate(0, raw0)
-        nc.scalar.copy(pairs[0][:, 1, :], window[1])
-        scatter(0)
-        group_w2(256, 384)
-        group_w2(384, 496)
-        activate(2, raw2)
-        nc.scalar.copy(pairs[1][:, 1, :], window[3])
-        scatter(2)
-        group_z(nc.scalar.copy, 0, 0)
-        group_z(nc.scalar.copy, 0, 1)
-        group_z(nc.scalar.copy, 0, 2)
+        def scatter(t, values):
+            nc.vector.tensor_tensor(window[t].indirect(take_sb[:]), values[:], wt_sb[:], MULT)
 
-        w2_codes = held.tile([P, N], U32, name="w2_codes", offset=4096, align_bytes=64)
-        w2_scale = keep.tile([P, N], U8, name="w2_scale", align_bytes=64)
-
-        def quantize_w2(half):
-            cols = slice(half * N // 2, (half + 1) * N // 2)
-            nc.vector.quantize_mx(
-                w2_codes[:, cols].bitcast(FP8X4), w2_scale[:, cols], w2_grouped[:, cols, :].rearrange("p c j -> p (c j)")
+        def group_w2(a, b):
+            by_scalar(
+                w2_grouped[:, a:b, :].rearrange("p (c i) j -> p c j i", i=4),
+                w2_raw[:, :, a:b].rearrange("p j (c i) -> p c j i", i=4),
             )
 
+        def group_z(copy, u, r):
+            a, b = RANGES[r]
+            copy(z_grouped[r][:, :, 2 * u : 2 * u + 2], pairs[u][:, :, a:b].rearrange("p s c -> p c s"))
+
+        activated_all = keep.tile([P, S], F32, name="activated_all")
+        for values, tokens in y[1]:
+            nc.scalar.activation(activated_all[:, tokens], values, GELU)
+        activated1 = fetch(1, activated_all[:])
+        fill_window(3)
+        raw3 = fetch(3, window[3])
+        fill_window(1)
+        scatter(1, activated1)
+        fill_window(0)
+        raw0 = fetch(0, window[0])
+        scatter(3, activate(3, raw3))
+        fill_window(2)
+        raw2 = fetch(2, window[2])
+        group_w2(0, P)
+        group_w2(P, 2 * P)
+        activated0 = activate(0, raw0)
+        by_scalar(pairs[0][:, 1, :], window[1])
+        scatter(0, activated0)
+        group_w2(2 * P, 3 * P)
+        group_w2(3 * P, N - W2_LATE)
+        activated2 = activate(2, raw2)
+        by_scalar(pairs[1][:, 1, :], window[3])
+        scatter(2, activated2)
+        for r in range(len(RANGES)):
+            group_z(by_scalar, 0, r)
+
+        w2_codes = keep.tile([P, N], U32, name="w2_codes", tag="scales_wt_w2", align_bytes=64)
+        w2_scale = keep.tile([P, N], U8, name="w2_scale", align_bytes=64)
         z_codes = keep.tile([P, S], U32, name="z_codes", align_bytes=64)
         z_scale = keep.tile([P, S], U8, name="z_scale", align_bytes=64)
 
-        def quantize_z(c):
-            a, b = CHUNKS[c]
-            nc.vector.quantize_mx(z_codes[:, a:b].bitcast(FP8X4), z_scale[:, a:b], z_grouped[c][:].rearrange("p c j -> p (c j)"))
+        def quantize_w2(a, b):
+            nc.vector.quantize_mx(
+                w2_codes[:, a:b].bitcast(FP8X4), w2_scale[:, a:b], w2_grouped[:, a:b, :].rearrange("p c j -> p (c j)")
+            )
+
+        def quantize_z(r):
+            a, b = RANGES[r]
+            nc.vector.quantize_mx(z_codes[:, a:b].bitcast(FP8X4), z_scale[:, a:b], z_grouped[r][:].rearrange("p c j -> p (c j)"))
+
+        group_z(by_vector, 1, 0)
+        group_z(by_scalar, 1, 1)
+        group_w2(N - W2_LATE, N)
+        group_z(by_scalar, 1, 2)
+        quantize_w2(0, N // 2)
+        quantize_z(0)
+        quantize_z(1)
+        quantize_w2(N // 2, N)
+        quantize_z(2)
 
         out_rows = out.rearrange("(mt p) j -> p mt j", p=P)
 
-        def second(mt, a, b, dest):
+        def second_product(mt, a, b, dest):
             nc.tensor.matmul_mx(
                 dest,
                 lhsT=w2_codes[:, mt * P : (mt + 1) * P].bitcast(FP8X4),
@@ -223,37 +211,24 @@ def tile_picked_modtrue_gelu_p_kernel(tc, x_words, x_scales, w1, wt, w2, offs, t
                 stop=True,
             )
 
-        def new_bank():
-            return psum.tile([P, S], F32, name="bank")
-
-        def store(mt, a, cuts, copy):
+        def result(mt, cuts, copy):
             bank = new_bank()
-            for lo, hi in zip(cuts, cuts[1:]):
-                second(mt, lo, hi, bank[:, lo - a : hi - a])
-            staged = keep.tile([P, HALF], F32, name=f"staged{mt}_{a}")
+            for a, b in zip(cuts, cuts[1:]):
+                second_product(mt, a, b, bank[:, a - cuts[0] : b - cuts[0]])
+            staged = keep.tile([P, HALF], F32, name=f"staged{mt}_{cuts[0]}")
             copy(staged[:], bank[:, 0:HALF])
-            nc.sync.dma_start(out_rows[:, mt, a : a + HALF], staged[:])
+            nc.sync.dma_start(out_rows[:, mt, cuts[0] : cuts[-1]], staged[:])
 
-        by_vector, by_scalar = nc.vector.tensor_copy, nc.scalar.copy
-        group_z(by_vector, 1, 0)
-        group_z(by_scalar, 1, 1)
-        group_w2(496, 512)
-        group_z(by_scalar, 1, 2)
-        quantize_w2(0)
-        quantize_z(0)
-        quantize_z(1)
-        quantize_w2(1)
-        quantize_z(2)
-        store(0, 0, (0, 128, 256), by_scalar)
-        store(1, 0, (0, 256), by_scalar)
-        store(2, 0, (0, 256), by_vector)
-        store(3, 0, (0, 256), by_scalar)
-        store(0, 256, (256, 512), by_vector)
-        store(1, 256, (256, 512), by_scalar)
-        store(2, 256, (256, 512), by_vector)
-        staged = keep.tile([P, HALF], F32, name="wide3")
+        result(0, (0, P, HALF), by_scalar)
+        result(1, (0, HALF), by_scalar)
+        result(2, (0, HALF), by_vector)
+        result(3, (0, HALF), by_scalar)
+        result(0, (HALF, S), by_vector)
+        result(1, (HALF, S), by_scalar)
+        result(2, (HALF, S), by_vector)
+        staged = keep.tile([P, HALF], F32, name="staged_last")
         for i, copy in enumerate((by_scalar, by_vector)):
             bank = new_bank()
-            second(3, 256 + i * P, 384 + i * P, bank[:, 0:P])
+            second_product(3, HALF + i * P, HALF + (i + 1) * P, bank[:, 0:P])
             copy(staged[:, i * P : (i + 1) * P], bank[:, 0:P])
-        nc.sync.dma_start(out_rows[:, 3, 256:512], staged[:])
+        nc.sync.dma_start(out_rows[:, 3, HALF:S], staged[:])

@@ -22,7 +22,7 @@ PACK = 4
 HALF = S // 2
 BANKS = 8
 RANGES = ((0, P), (P, HALF), (HALF, S))
-W2_LATE = 16
+W2_LATE = 4
 
 
 def tile_picked_modtrue_gelu_p_kernel(tc, x_words, x_scales, w1, wt, w2, offs, take, out):
@@ -220,14 +220,14 @@ def tile_picked_modtrue_gelu_p_kernel(tc, x_words, x_scales, w1, wt, w2, offs, t
             nc.sync.dma_start(out_rows[:, mt, cuts[0] : cuts[-1]], staged[:])
 
         result(0, (0, P, HALF), by_scalar)
-        result(1, (0, HALF), by_scalar)
-        result(2, (0, HALF), by_vector)
-        result(3, (0, HALF), by_scalar)
-        result(0, (HALF, S), by_vector)
-        result(1, (HALF, S), by_scalar)
-        result(2, (HALF, S), by_vector)
+        result(1, (0, HALF), by_vector)
+        result(2, (0, HALF), by_scalar)
+        result(3, (0, HALF), by_vector)
+        result(0, (HALF, S), by_scalar)
+        result(1, (HALF, S), by_vector)
+        result(2, (HALF, S), by_scalar)
         staged = keep.tile([P, HALF], F32, name="staged_last")
-        for i, copy in enumerate((by_scalar, by_vector)):
+        for i, copy in enumerate((by_vector, by_scalar)):
             bank = new_bank()
             second_product(3, HALF + i * P, HALF + (i + 1) * P, bank[:, 0:P])
             copy(staged[:, i * P : (i + 1) * P], bank[:, 0:P])

@@ -15,7 +15,9 @@ U16 = mybir.dt.uint16
 U8 = mybir.dt.uint8
 FP8X4 = mybir.dt.float8_e4m3fn_x4
 GELU = mybir.ActivationFunctionType.Gelu_apprx_tanh
+COPY = mybir.ActivationFunctionType.Copy
 MULT = mybir.AluOpType.mult
+ADD = mybir.AluOpType.add
 
 P = 128
 PACK = 4
@@ -118,16 +120,26 @@ def tile_picked_modtrue_gelu_p_kernel(tc, x_words, x_scales, w1, wt, w2, offs, t
         for u in range(2):
             window[2 * u] = pairs[u][:].rearrange("p s c -> p (s c)")
             window[2 * u + 1] = keep.tile([P, S], F32, name=f"single{u}")[:]
-        w2_grouped = keep.tile([P, N, PACK], BF16, name="w2_grouped", align_bytes=64)
         z_grouped = [keep.tile([P, b - a, PACK], BF16, name=f"z_grouped{a}", align_bytes=64) for a, b in RANGES]
 
         def fill_window(t):
             for values, tokens in y[t]:
                 by_scalar(window[t][:, tokens], values)
 
-        def fetch(t, source):
-            got = keep.tile([P, V], F32, name=f"got{t}")
-            by_vector(got[:], source.indirect(take_sb[:]))
+        def activate_all(t):
+            done = keep.tile([P, S], F32, name=f"activated{t}", tag=f"activated_then_w2_{t}", align_bytes=64)
+            for values, tokens in y[t]:
+                nc.scalar.activation(done[:, tokens], values, GELU)
+            return done
+
+        def fetch_weighted(t, activated):
+            got = keep.tile([P, V], F32, name=f"weighted{t}")
+            nc.vector.tensor_tensor(got[:], activated[:].indirect(take_sb[:]), wt_sb[:], MULT)
+            return got
+
+        def fetch_raw(t):
+            got = keep.tile([P, V], F32, name=f"raw{t}")
+            nc.scalar.activation(got[:], window[t].indirect(take_sb[:]), COPY)
             return got
 
         def activate(t, raw):
@@ -136,6 +148,9 @@ def tile_picked_modtrue_gelu_p_kernel(tc, x_words, x_scales, w1, wt, w2, offs, t
             return done
 
         def scatter(t, values):
+            by_vector(window[t].indirect(take_sb[:]), values[:])
+
+        def scatter_weighted(t, values):
             nc.vector.tensor_tensor(window[t].indirect(take_sb[:]), values[:], wt_sb[:], MULT)
 
         def group_w2(a, b):
@@ -148,29 +163,27 @@ def tile_picked_modtrue_gelu_p_kernel(tc, x_words, x_scales, w1, wt, w2, offs, t
             a, b = RANGES[r]
             copy(z_grouped[r][:, :, 2 * u : 2 * u + 2], pairs[u][:, :, a:b].rearrange("p s c -> p c s"))
 
-        activated_all = keep.tile([P, S], F32, name="activated_all")
-        for values, tokens in y[1]:
-            nc.scalar.activation(activated_all[:, tokens], values, GELU)
-        activated1 = fetch(1, activated_all[:])
-        fill_window(3)
-        raw3 = fetch(3, window[3])
+        activated1 = activate_all(1)
+        weighted1 = fetch_weighted(1, activated1)
+        activated3 = activate_all(3)
+        weighted3 = fetch_weighted(3, activated3)
         fill_window(1)
-        scatter(1, activated1)
+        scatter(1, weighted1)
+        w2_grouped = keep.tile([P, N, PACK], BF16, name="w2_grouped", tag="activated_then_w2_3", align_bytes=64)
+        nc.gpsimd.tensor_scalar(
+            w2_grouped[:, 0 : 3 * P, :], w2_raw[:, :, 0 : 3 * P].rearrange("p j c -> p c j"), 1.0, 0.0, MULT, ADD
+        )
+        fill_window(3)
+        scatter(3, weighted3)
         fill_window(0)
-        raw0 = fetch(0, window[0])
-        scatter(3, activate(3, raw3))
-        fill_window(2)
-        raw2 = fetch(2, window[2])
-        group_w2(0, P)
-        group_w2(P, 2 * P)
-        activated0 = activate(0, raw0)
+        raw0 = fetch_raw(0)
         by_scalar(pairs[0][:, 1, :], window[1])
-        scatter(0, activated0)
-        group_w2(2 * P, 3 * P)
-        group_w2(3 * P, N - W2_LATE)
-        activated2 = activate(2, raw2)
+        fill_window(2)
+        scatter_weighted(0, activate(0, raw0))
+        raw2 = fetch_raw(2)
         by_scalar(pairs[1][:, 1, :], window[3])
-        scatter(2, activated2)
+        scatter_weighted(2, activate(2, raw2))
+        group_w2(3 * P, N - W2_LATE)
         for r in range(len(RANGES)):
             group_z(by_scalar, 0, r)
 
@@ -179,9 +192,10 @@ def tile_picked_modtrue_gelu_p_kernel(tc, x_words, x_scales, w1, wt, w2, offs, t
         z_codes = keep.tile([P, S], U32, name="z_codes", align_bytes=64)
         z_scale = keep.tile([P, S], U8, name="z_scale", align_bytes=64)
 
-        def quantize_w2(a, b):
+        def quantize_w2(h):
+            cols = slice(h * HALF, (h + 1) * HALF)
             nc.vector.quantize_mx(
-                w2_codes[:, a:b].bitcast(FP8X4), w2_scale[:, a:b], w2_grouped[:, a:b, :].rearrange("p c j -> p (c j)")
+                w2_codes[:, cols].bitcast(FP8X4), w2_scale[:, cols], w2_grouped[:, cols, :].rearrange("p c j -> p (c j)")
             )
 
         def quantize_z(r):
@@ -192,10 +206,10 @@ def tile_picked_modtrue_gelu_p_kernel(tc, x_words, x_scales, w1, wt, w2, offs, t
         group_z(by_scalar, 1, 1)
         group_w2(N - W2_LATE, N)
         group_z(by_scalar, 1, 2)
-        quantize_w2(0, N // 2)
+        quantize_w2(0)
         quantize_z(0)
         quantize_z(1)
-        quantize_w2(N // 2, N)
+        quantize_w2(1)
         quantize_z(2)
 
         out_rows = out.rearrange("(mt p) j -> p mt j", p=P)

@@ -176,13 +176,14 @@ def tile_picked_modtrue_gelu_p_kernel(tc, x_words, x_scales, w1, wt, w2, offs, t
         fill_window(3)
         scatter(3, weighted3)
         fill_window(0)
-        raw0 = fetch_raw(0)
-        by_scalar(pairs[0][:, 1, :], window[1])
         fill_window(2)
-        scatter_weighted(0, activate(0, raw0))
+        raw0 = fetch_raw(0)
         raw2 = fetch_raw(2)
+        nc.gpsimd.tensor_scalar(pairs[0][:, 1, :], window[1], 1.0, 0.0, MULT, ADD)
+        scatter_weighted(0, activate(0, raw0))
+        activated2 = activate(2, raw2)
         by_scalar(pairs[1][:, 1, :], window[3])
-        scatter_weighted(2, activate(2, raw2))
+        scatter_weighted(2, activated2)
         group_w2(3 * P, N - W2_LATE)
         for r in range(len(RANGES)):
             group_z(by_scalar, 0, r)

@@ -40,11 +40,10 @@ def tile_picked_modtrue_gelu_p_kernel(tc, x_words, x_scales, w1, wt, w2, offs, t
         take_sb = lists.tile([P, V // 16], U16, name="take_sb")
 
         scale_table = keep.tile([P, T], U8, name="scale_table", tag="scales_wt_w2", align_bytes=64)
-        for a, b in ((0, 16), (32, 64), (64, P)):
-            nc.vector.memset(scale_table[a:b, :].bitcast(I32), 0)
+        nc.vector.memset(scale_table[0 : P - 16, :].bitcast(I32), 0)
         x_scale = keep.tile([P, S], U8, name="x_scale", align_bytes=64)
         nc.vector.memset(x_scale[:].bitcast(I32), 0)
-        nc.scalar.dma_start(scale_table[16:32, :].bitcast(I32), x_scales[0].bitcast(I32))
+        nc.scalar.dma_start(scale_table[P - 16 : P, :].bitcast(I32), x_scales[0].bitcast(I32))
         nc.sync.dma_start(offs_sb[:], offs)
 
         word_table = keep.tile([P, T], U32, name="word_table", tag="words_then_w2", align_bytes=64)
@@ -58,7 +57,7 @@ def tile_picked_modtrue_gelu_p_kernel(tc, x_words, x_scales, w1, wt, w2, offs, t
         picked_scale = keep.tile([P, S], U8, name="picked_scale", align_bytes=64)
         by_vector(picked_scale[:], scale_table[:].indirect(offs_sb[:]))
         for q in range(4):
-            nc.scalar.dma_start(x_scale[32 * q : 32 * q + 4, :].bitcast(I32), picked_scale[16 + 4 * q : 20 + 4 * q, :].bitcast(I32))
+            nc.scalar.dma_start(x_scale[32 * q : 32 * q + 4, :].bitcast(I32), picked_scale[P - 16 + 4 * q : P - 12 + 4 * q, :].bitcast(I32))
         wt_sb = keep.tile([P, V], F32, name="wt_sb", tag="scales_wt_w2", align_bytes=64)
         nc.sync.dma_start(wt_sb[:], wt.rearrange("(p j) v -> p j v", j=PACK)[:, 0, :])
 
@@ -173,11 +172,12 @@ def tile_picked_modtrue_gelu_p_kernel(tc, x_words, x_scales, w1, wt, w2, offs, t
         nc.gpsimd.tensor_scalar(
             w2_grouped[:, 0 : 3 * P, :], w2_raw[:, :, 0 : 3 * P].rearrange("p j c -> p c j"), 1.0, 0.0, MULT, ADD
         )
+        fill_window(0)
+        raw0 = keep.tile([P, V], F32, name="raw0")
+        by_vector(raw0[:], window[0].indirect(take_sb[:]))
+        fill_window(2)
         fill_window(3)
         scatter(3, weighted3)
-        fill_window(0)
-        fill_window(2)
-        raw0 = fetch_raw(0)
         raw2 = fetch_raw(2)
         nc.gpsimd.tensor_scalar(pairs[0][:, 1, :], window[1], 1.0, 0.0, MULT, ADD)
         scatter_weighted(0, activate(0, raw0))

@@ -46,6 +46,19 @@ def tile_picked_modtrue_gelu_p_kernel(tc, x_words, x_scales, w1, wt, w2, offs, t
         nc.scalar.dma_start(scale_table[P - 16 : P, :].bitcast(I32), x_scales[0].bitcast(I32))
         nc.sync.dma_start(offs_sb[:], offs)
 
+        warm = keep.tile([P, 2, 32], F32, name="warm", align_bytes=256)
+        warm_rounded = keep.tile([P, P], BF16, name="warm_rounded", align_bytes=256)
+        nc.gpsimd.memset(warm[:, 0, :], 0.0)
+        nc.gpsimd.tensor_scalar(warm[:, 1, :], warm[:, 0, :], 1.0, 0.0, MULT, ADD)
+        nc.gpsimd.tensor_scalar(
+            warm_rounded[:, 0:32].rearrange("p (c j) -> p c j", j=PACK),
+            warm[:, 0, :].rearrange("p (j c) -> p c j", j=PACK),
+            1.0,
+            0.0,
+            MULT,
+            ADD,
+        )
+
         word_table = keep.tile([P, T], U32, name="word_table", tag="words_then_w2", align_bytes=64)
         nc.sync.dma_start(word_table[:].bitcast(I32), x_words[0].rearrange("p n r -> p (n r)").bitcast(I32))
         w1_rows = w1.rearrange("(p j) c -> p j c", j=PACK)

@@ -25,14 +25,21 @@ HALF = S // 2
 BANKS = 8
 RANGES = ((0, P), (P, HALF), (HALF, S))
 W2_LATE = 4
+W2_GPSIMD = 3 * P
+WARM = 8
 
 
 def tile_picked_modtrue_gelu_p_kernel(tc, x_words, x_scales, w1, wt, w2, offs, take, out):
     nc = tc.nc
     by_vector, by_scalar = nc.vector.tensor_copy, nc.scalar.copy
+
+    def group_by_gpsimd(grouped, rows):
+        nc.gpsimd.tensor_scalar(grouped, rows.rearrange("p j c -> p c j"), 1.0, 0.0, MULT, ADD)
+
     with ExitStack() as ctx:
         lists = ctx.enter_context(tc.tile_pool(name="lists", bufs=1))
         keep = ctx.enter_context(tc.tile_pool(name="keep", bufs=1))
+        spare = ctx.enter_context(tc.tile_pool(name="spare", bufs=1))
         psum = ctx.enter_context(tc.psum_pool(name="psum", bufs=BANKS))
 
 
@@ -40,24 +47,17 @@ def tile_picked_modtrue_gelu_p_kernel(tc, x_words, x_scales, w1, wt, w2, offs, t
         take_sb = lists.tile([P, V // 16], U16, name="take_sb")
 
         scale_table = keep.tile([P, T], U8, name="scale_table", tag="scales_wt_w2", align_bytes=64)
-        nc.vector.memset(scale_table[0 : P - 16, :].bitcast(I32), 0)
+        for a, b in ((0, 16), (32, 64), (64, P)):
+            nc.vector.memset(scale_table[a:b, :].bitcast(I32), 0)
         x_scale = keep.tile([P, S], U8, name="x_scale", align_bytes=64)
         nc.vector.memset(x_scale[:].bitcast(I32), 0)
-        nc.scalar.dma_start(scale_table[P - 16 : P, :].bitcast(I32), x_scales[0].bitcast(I32))
+        nc.scalar.dma_start(scale_table[16:32, :].bitcast(I32), x_scales[0].bitcast(I32))
         nc.sync.dma_start(offs_sb[:], offs)
 
-        warm = keep.tile([P, 2, 32], F32, name="warm", align_bytes=256)
-        warm_rounded = keep.tile([P, P], BF16, name="warm_rounded", align_bytes=256)
-        nc.gpsimd.memset(warm[:, 0, :], 0.0)
-        nc.gpsimd.tensor_scalar(warm[:, 1, :], warm[:, 0, :], 1.0, 0.0, MULT, ADD)
-        nc.gpsimd.tensor_scalar(
-            warm_rounded[:, 0:32].rearrange("p (c j) -> p c j", j=PACK),
-            warm[:, 0, :].rearrange("p (j c) -> p c j", j=PACK),
-            1.0,
-            0.0,
-            MULT,
-            ADD,
-        )
+        warm_in = spare.tile([P, PACK, WARM], F32, name="warm_in")
+        warm_out = spare.tile([P, WARM, PACK], BF16, name="warm_out")
+        nc.gpsimd.memset(warm_in[:], 0.0)
+        group_by_gpsimd(warm_out[:], warm_in[:])
 
         word_table = keep.tile([P, T], U32, name="word_table", tag="words_then_w2", align_bytes=64)
         nc.sync.dma_start(word_table[:].bitcast(I32), x_words[0].rearrange("p n r -> p (n r)").bitcast(I32))
@@ -70,7 +70,7 @@ def tile_picked_modtrue_gelu_p_kernel(tc, x_words, x_scales, w1, wt, w2, offs, t
         picked_scale = keep.tile([P, S], U8, name="picked_scale", align_bytes=64)
         by_vector(picked_scale[:], scale_table[:].indirect(offs_sb[:]))
         for q in range(4):
-            nc.scalar.dma_start(x_scale[32 * q : 32 * q + 4, :].bitcast(I32), picked_scale[P - 16 + 4 * q : P - 12 + 4 * q, :].bitcast(I32))
+            nc.scalar.dma_start(x_scale[32 * q : 32 * q + 4, :].bitcast(I32), picked_scale[16 + 4 * q : 20 + 4 * q, :].bitcast(I32))
         wt_sb = keep.tile([P, V], F32, name="wt_sb", tag="scales_wt_w2", align_bytes=64)
         nc.sync.dma_start(wt_sb[:], wt.rearrange("(p j) v -> p j v", j=PACK)[:, 0, :])
 
@@ -182,9 +182,7 @@ def tile_picked_modtrue_gelu_p_kernel(tc, x_words, x_scales, w1, wt, w2, offs, t
         fill_window(1)
         scatter(1, weighted1)
         w2_grouped = keep.tile([P, N, PACK], BF16, name="w2_grouped", tag="activated_then_w2_3", align_bytes=64)
-        nc.gpsimd.tensor_scalar(
-            w2_grouped[:, 0 : 3 * P, :], w2_raw[:, :, 0 : 3 * P].rearrange("p j c -> p c j"), 1.0, 0.0, MULT, ADD
-        )
+        group_by_gpsimd(w2_grouped[:, 0:W2_GPSIMD, :], w2_raw[:, :, 0:W2_GPSIMD])
         fill_window(0)
         raw0 = keep.tile([P, V], F32, name="raw0")
         by_vector(raw0[:], window[0].indirect(take_sb[:]))
@@ -192,12 +190,13 @@ def tile_picked_modtrue_gelu_p_kernel(tc, x_words, x_scales, w1, wt, w2, offs, t
         fill_window(3)
         scatter(3, weighted3)
         raw2 = fetch_raw(2)
-        nc.gpsimd.tensor_scalar(pairs[0][:, 1, :], window[1], 1.0, 0.0, MULT, ADD)
-        scatter_weighted(0, activate(0, raw0))
+        activated0 = activate(0, raw0)
+        by_scalar(pairs[0][:, 1, :], window[1])
+        scatter_weighted(0, activated0)
         activated2 = activate(2, raw2)
         by_scalar(pairs[1][:, 1, :], window[3])
         scatter_weighted(2, activated2)
-        group_w2(3 * P, N - W2_LATE)
+        group_w2(W2_GPSIMD, N - W2_LATE)
         for r in range(len(RANGES)):
             group_z(by_scalar, 0, r)
 

@@ -25,7 +25,7 @@ HALF = S // 2
 BANKS = 8
 RANGES = ((0, P), (P, HALF), (HALF, S))
 W2_LATE = 4
-W2_GPSIMD = 3 * P
+W2_GPSIMD = 320
 WARM = 8
 
 
@@ -183,20 +183,18 @@ def tile_picked_modtrue_gelu_p_kernel(tc, x_words, x_scales, w1, wt, w2, offs, t
         scatter(1, weighted1)
         w2_grouped = keep.tile([P, N, PACK], BF16, name="w2_grouped", tag="activated_then_w2_3", align_bytes=64)
         group_by_gpsimd(w2_grouped[:, 0:W2_GPSIMD, :], w2_raw[:, :, 0:W2_GPSIMD])
-        fill_window(0)
-        raw0 = keep.tile([P, V], F32, name="raw0")
-        by_vector(raw0[:], window[0].indirect(take_sb[:]))
-        fill_window(2)
         fill_window(3)
         scatter(3, weighted3)
+        fill_window(0)
+        fill_window(2)
+        raw0 = fetch_raw(0)
         raw2 = fetch_raw(2)
-        activated0 = activate(0, raw0)
-        by_scalar(pairs[0][:, 1, :], window[1])
-        scatter_weighted(0, activated0)
+        nc.gpsimd.tensor_scalar(pairs[0][:, 1, :], window[1], 1.0, 0.0, MULT, ADD)
+        scatter_weighted(0, activate(0, raw0))
         activated2 = activate(2, raw2)
+        group_w2(W2_GPSIMD, N - W2_LATE)
         by_scalar(pairs[1][:, 1, :], window[3])
         scatter_weighted(2, activated2)
-        group_w2(W2_GPSIMD, N - W2_LATE)
         for r in range(len(RANGES)):
             group_z(by_scalar, 0, r)
 

@@ -25,7 +25,7 @@ HALF = S // 2
 BANKS = 8
 RANGES = ((0, P), (P, HALF), (HALF, S))
 W2_LATE = 4
-W2_GPSIMD = 320
+W2_GPSIMD = 3 * P
 WARM = 8
 
 
@@ -47,11 +47,11 @@ def tile_picked_modtrue_gelu_p_kernel(tc, x_words, x_scales, w1, wt, w2, offs, t
         take_sb = lists.tile([P, V // 16], U16, name="take_sb")
 
         scale_table = keep.tile([P, T], U8, name="scale_table", tag="scales_wt_w2", align_bytes=64)
-        for a, b in ((0, 16), (32, 64), (64, P)):
+        for a, b in ((0, 48), (64, P)):
             nc.vector.memset(scale_table[a:b, :].bitcast(I32), 0)
         x_scale = keep.tile([P, S], U8, name="x_scale", align_bytes=64)
         nc.vector.memset(x_scale[:].bitcast(I32), 0)
-        nc.scalar.dma_start(scale_table[16:32, :].bitcast(I32), x_scales[0].bitcast(I32))
+        nc.scalar.dma_start(scale_table[48:64, :].bitcast(I32), x_scales[0].bitcast(I32))
         nc.sync.dma_start(offs_sb[:], offs)
 
         warm_in = spare.tile([P, PACK, WARM], F32, name="warm_in")
@@ -70,7 +70,7 @@ def tile_picked_modtrue_gelu_p_kernel(tc, x_words, x_scales, w1, wt, w2, offs, t
         picked_scale = keep.tile([P, S], U8, name="picked_scale", align_bytes=64)
         by_vector(picked_scale[:], scale_table[:].indirect(offs_sb[:]))
         for q in range(4):
-            nc.scalar.dma_start(x_scale[32 * q : 32 * q + 4, :].bitcast(I32), picked_scale[16 + 4 * q : 20 + 4 * q, :].bitcast(I32))
+            nc.scalar.dma_start(x_scale[32 * q : 32 * q + 4, :].bitcast(I32), picked_scale[48 + 4 * q : 52 + 4 * q, :].bitcast(I32))
         wt_sb = keep.tile([P, V], F32, name="wt_sb", tag="scales_wt_w2", align_bytes=64)
         nc.sync.dma_start(wt_sb[:], wt.rearrange("(p j) v -> p j v", j=PACK)[:, 0, :])
 
@@ -93,17 +93,20 @@ def tile_picked_modtrue_gelu_p_kernel(tc, x_words, x_scales, w1, wt, w2, offs, t
         odd_cols = odd[:].rearrange("p u m j -> p m u j")
         by_vector(odd_cols[:, :, :, 0:2], w1_cols[:, 1, :, :, 0:2])
         by_vector(odd_cols[:, :, :, 2], w1_cols[:, 1, :, :, 2])
-        for u in range(2):
-            by_vector(odd_cols[:, :, u, 3], w1_cols[:, 1, :, u, 3])
-        for u in range(2):
-            quantize_w1(1, odd, u, 0, P)
-        even = keep.tile([P, 2, P, PACK], BF16, name="w1_even", tag="w1_grouped", align_bytes=64)
         column_halves = ((0, P // 2), (P // 2, P))
         for a, b in column_halves:
-            by_vector(even[:].rearrange("p u m j -> p m u j")[:, a:b], w1_cols[:, 0, a:b])
+            by_vector(odd_cols[:, a:b, 0, 3], w1_cols[:, 1, a:b, 0, 3])
         for a, b in column_halves:
-            for u in range(2):
-                quantize_w1(0, even, u, a, b)
+            quantize_w1(1, odd, 0, a, b)
+        by_vector(odd_cols[:, :, 1, 3], w1_cols[:, 1, :, 1, 3])
+        quantize_w1(1, odd, 1, 0, P)
+        warm_gelu = spare.tile([P, 1], F32, name="warm_gelu")
+        nc.scalar.activation(warm_gelu[:], w1_raw[:, 0, 0:1], GELU)
+        even = keep.tile([P, 2, P, PACK], BF16, name="w1_even", align_bytes=64)
+        for a, b in ((0, 2), (2, 4)):
+            by_scalar(even[:].rearrange("p u m j -> p m u j")[:, :, :, a:b], w1_cols[:, 0, :, :, a:b])
+        for u in range(2):
+            quantize_w1(0, even, u, 0, P)
 
         def new_bank():
             return psum.tile([P, S], F32, name="bank")
@@ -134,9 +137,9 @@ def tile_picked_modtrue_gelu_p_kernel(tc, x_words, x_scales, w1, wt, w2, offs, t
             window[2 * u + 1] = keep.tile([P, S], F32, name=f"single{u}")[:]
         z_grouped = [keep.tile([P, b - a, PACK], BF16, name=f"z_grouped{a}", align_bytes=64) for a, b in RANGES]
 
-        def fill_window(t):
-            for values, tokens in y[t]:
-                by_scalar(window[t][:, tokens], values)
+        def fill_window(t, copy=by_scalar, parts=slice(None)):
+            for values, tokens in y[t][parts]:
+                copy(window[t][:, tokens], values)
 
         def activate_all(t):
             done = keep.tile([P, S], F32, name=f"activated{t}", tag=f"activated_then_w2_{t}", align_bytes=64)
@@ -176,23 +179,25 @@ def tile_picked_modtrue_gelu_p_kernel(tc, x_words, x_scales, w1, wt, w2, offs, t
             copy(z_grouped[r][:, :, 2 * u : 2 * u + 2], pairs[u][:, :, a:b].rearrange("p s c -> p c s"))
 
         activated1 = activate_all(1)
+        fill_window(1, by_vector, slice(0, 3))
         weighted1 = fetch_weighted(1, activated1)
         activated3 = activate_all(3)
         weighted3 = fetch_weighted(3, activated3)
-        fill_window(1)
+        fill_window(1, by_scalar, slice(3, 4))
         scatter(1, weighted1)
         w2_grouped = keep.tile([P, N, PACK], BF16, name="w2_grouped", tag="activated_then_w2_3", align_bytes=64)
         group_by_gpsimd(w2_grouped[:, 0:W2_GPSIMD, :], w2_raw[:, :, 0:W2_GPSIMD])
+        fill_window(0)
         fill_window(3)
         scatter(3, weighted3)
-        fill_window(0)
-        fill_window(2)
         raw0 = fetch_raw(0)
+        fill_window(2)
+        activated0 = activate(0, raw0)
+        by_scalar(pairs[0][:, 1, :], window[1])
+        scatter_weighted(0, activated0)
         raw2 = fetch_raw(2)
-        nc.gpsimd.tensor_scalar(pairs[0][:, 1, :], window[1], 1.0, 0.0, MULT, ADD)
-        scatter_weighted(0, activate(0, raw0))
-        activated2 = activate(2, raw2)
         group_w2(W2_GPSIMD, N - W2_LATE)
+        activated2 = activate(2, raw2)
         by_scalar(pairs[1][:, 1, :], window[3])
         scatter_weighted(2, activated2)
         for r in range(len(RANGES)):

@@ -25,7 +25,7 @@ HALF = S // 2
 BANKS = 8
 RANGES = ((0, P), (P, HALF), (HALF, S))
 W2_LATE = 4
-W2_GPSIMD = 3 * P
+W2_GPSIMD = 3 * P // 2
 WARM = 8
 
 
@@ -77,7 +77,8 @@ def tile_picked_modtrue_gelu_p_kernel(tc, x_words, x_scales, w1, wt, w2, offs, t
         x_codes = keep.tile([P, S], U32, name="x_codes", align_bytes=64)
         by_vector(x_codes[:], word_table[:].indirect(offs_sb[:]))
         w2_raw = keep.tile([P, PACK, N], F32, name="w2_raw", tag="words_then_w2", align_bytes=64)
-        nc.sync.dma_start(w2_raw[:], w2.rearrange("(p j) c -> p j c", j=PACK))
+        for a in (0, HALF):
+            nc.sync.dma_start(w2_raw[:, :, a : a + HALF], w2.rearrange("(p j) c -> p j c", j=PACK)[:, :, a : a + HALF])
 
         w1_cols = w1_raw[:].rearrange("p j (m u e) -> p e m u j", u=2, e=2)
         w1_codes = {e: keep.tile([P, H // 2], U32, name=f"w1_codes{e}", align_bytes=64) for e in (1, 0)}
@@ -153,7 +154,7 @@ def tile_picked_modtrue_gelu_p_kernel(tc, x_words, x_scales, w1, wt, w2, offs, t
             return got
 
         def fetch_raw(t):
-            got = keep.tile([P, V], F32, name=f"raw{t}")
+            got = keep.tile([P, V], F32, name=f"raw{t}", tag=f"raw_then_w2_{t}", align_bytes=64)
             nc.scalar.activation(got[:], window[t].indirect(take_sb[:]), COPY)
             return got
 
@@ -170,7 +171,7 @@ def tile_picked_modtrue_gelu_p_kernel(tc, x_words, x_scales, w1, wt, w2, offs, t
 
         def group_w2(a, b):
             by_scalar(
-                w2_grouped[:, a:b, :].rearrange("p (c i) j -> p c j i", i=4),
+                w2_grouped[a // HALF][:, a % HALF : a % HALF + b - a, :].rearrange("p (c i) j -> p c j i", i=4),
                 w2_raw[:, :, a:b].rearrange("p j (c i) -> p c j i", i=4),
             )
 
@@ -185,20 +186,22 @@ def tile_picked_modtrue_gelu_p_kernel(tc, x_words, x_scales, w1, wt, w2, offs, t
         weighted3 = fetch_weighted(3, activated3)
         fill_window(1, by_scalar, slice(3, 4))
         scatter(1, weighted1)
-        w2_grouped = keep.tile([P, N, PACK], BF16, name="w2_grouped", tag="activated_then_w2_3", align_bytes=64)
-        group_by_gpsimd(w2_grouped[:, 0:W2_GPSIMD, :], w2_raw[:, :, 0:W2_GPSIMD])
+        w2_grouped = [keep.tile([P, HALF, PACK], BF16, name="w2_grouped0", tag="activated_then_w2_3", align_bytes=64)]
+        group_by_gpsimd(w2_grouped[0][:, 0:W2_GPSIMD, :], w2_raw[:, :, 0:W2_GPSIMD])
         fill_window(0)
         fill_window(3)
         scatter(3, weighted3)
         raw0 = fetch_raw(0)
         fill_window(2)
         activated0 = activate(0, raw0)
-        by_scalar(pairs[0][:, 1, :], window[1])
+        nc.gpsimd.tensor_scalar(pairs[0][:, 1, :], window[1], 1.0, 0.0, MULT, ADD)
         scatter_weighted(0, activated0)
         raw2 = fetch_raw(2)
-        group_w2(W2_GPSIMD, N - W2_LATE)
+        group_w2(W2_GPSIMD, HALF)
         activated2 = activate(2, raw2)
         by_scalar(pairs[1][:, 1, :], window[3])
+        w2_grouped.append(keep.tile([P, HALF, PACK], BF16, name="w2_grouped1", tag="raw_then_w2_2", align_bytes=64))
+        group_w2(HALF, N - W2_LATE)
         scatter_weighted(2, activated2)
         for r in range(len(RANGES)):
             group_z(by_scalar, 0, r)
@@ -211,7 +214,7 @@ def tile_picked_modtrue_gelu_p_kernel(tc, x_words, x_scales, w1, wt, w2, offs, t
         def quantize_w2(h):
             cols = slice(h * HALF, (h + 1) * HALF)
             nc.vector.quantize_mx(
-                w2_codes[:, cols].bitcast(FP8X4), w2_scale[:, cols], w2_grouped[:, cols, :].rearrange("p c j -> p (c j)")
+                w2_codes[:, cols].bitcast(FP8X4), w2_scale[:, cols], w2_grouped[h][:].rearrange("p c j -> p (c j)")
             )
 
         def quantize_z(r):

@@ -135,8 +135,7 @@ def tile_picked_modtrue_gelu_p_kernel(tc, x_words, x_scales, w1, wt, w2, offs, t
         window = {}
         for u in range(2):
             window[2 * u] = pairs[u][:].rearrange("p s c -> p (s c)")
-            window[2 * u + 1] = keep.tile([P, S], F32, name=f"single{u}")[:]
-        z_grouped = [keep.tile([P, b - a, PACK], BF16, name=f"z_grouped{a}", align_bytes=64) for a, b in RANGES]
+            window[2 * u + 1] = keep.tile([P, S], F32, name=f"single{u}", tag=f"single_then_z_{u}", align_bytes=64)[:]
 
         def fill_window(t, copy=by_scalar, parts=slice(None)):
             for values, tokens in y[t][parts]:
@@ -175,9 +174,11 @@ def tile_picked_modtrue_gelu_p_kernel(tc, x_words, x_scales, w1, wt, w2, offs, t
                 w2_raw[:, :, a:b].rearrange("p j (c i) -> p c j i", i=4),
             )
 
-        def group_z(copy, u, r):
-            a, b = RANGES[r]
-            copy(z_grouped[r][:, :, 2 * u : 2 * u + 2], pairs[u][:, :, a:b].rearrange("p s c -> p c s"))
+        def z_grouped(a, b):
+            return z_first[:, a:b, :] if b <= P else z_rest[:, a - P : b - P, :]
+
+        def group_z(copy, u, a, b):
+            copy(z_grouped(a, b)[:, :, 2 * u : 2 * u + 2], pairs[u][:, :, a:b].rearrange("p s c -> p c s"))
 
         activated1 = activate_all(1)
         fill_window(1, by_vector, slice(0, 3))
@@ -203,8 +204,10 @@ def tile_picked_modtrue_gelu_p_kernel(tc, x_words, x_scales, w1, wt, w2, offs, t
         w2_grouped.append(keep.tile([P, HALF, PACK], BF16, name="w2_grouped1", tag="raw_then_w2_2", align_bytes=64))
         group_w2(HALF, N - W2_LATE)
         scatter_weighted(2, activated2)
-        for r in range(len(RANGES)):
-            group_z(by_scalar, 0, r)
+        z_first = keep.tile([P, P, PACK], BF16, name="z_first", tag="single_then_z_1", align_bytes=64)
+        z_rest = keep.tile([P, S - P, PACK], BF16, name="z_rest", align_bytes=64)
+        group_z(by_vector, 0, 0, P)
+        group_z(by_scalar, 0, P, S)
 
         w2_codes = keep.tile([P, N], U32, name="w2_codes", tag="scales_wt_w2", align_bytes=64)
         w2_scale = keep.tile([P, N], U8, name="w2_scale", align_bytes=64)
@@ -219,12 +222,12 @@ def tile_picked_modtrue_gelu_p_kernel(tc, x_words, x_scales, w1, wt, w2, offs, t
 
         def quantize_z(r):
             a, b = RANGES[r]
-            nc.vector.quantize_mx(z_codes[:, a:b].bitcast(FP8X4), z_scale[:, a:b], z_grouped[r][:].rearrange("p c j -> p (c j)"))
+            nc.vector.quantize_mx(z_codes[:, a:b].bitcast(FP8X4), z_scale[:, a:b], z_grouped(a, b).rearrange("p c j -> p (c j)"))
 
-        group_z(by_vector, 1, 0)
-        group_z(by_scalar, 1, 1)
+        group_z(by_vector, 1, *RANGES[0])
+        group_z(by_scalar, 1, *RANGES[1])
         group_w2(N - W2_LATE, N)
-        group_z(by_scalar, 1, 2)
+        group_z(by_scalar, 1, *RANGES[2])
         quantize_w2(0)
         quantize_z(0)
         quantize_z(1)
@@ -248,11 +251,12 @@ def tile_picked_modtrue_gelu_p_kernel(tc, x_words, x_scales, w1, wt, w2, offs, t
             bank = new_bank()
             for a, b in zip(cuts, cuts[1:]):
                 second_product(mt, a, b, bank[:, a - cuts[0] : b - cuts[0]])
-            staged = keep.tile([P, HALF], F32, name=f"staged{mt}_{cuts[0]}")
-            copy(staged[:], bank[:, 0:HALF])
+            staged = keep.tile([P, cuts[-1] - cuts[0]], F32, name=f"staged{mt}_{cuts[0]}")
+            copy(staged[:], bank[:, 0 : cuts[-1] - cuts[0]])
             nc.sync.dma_start(out_rows[:, mt, cuts[0] : cuts[-1]], staged[:])
 
-        result(0, (0, P, HALF), by_scalar)
+        result(0, (0, P), by_scalar)
+        result(0, (P, HALF), by_scalar)
         result(1, (0, HALF), by_vector)
         result(2, (0, HALF), by_scalar)
         result(3, (0, HALF), by_vector)

@@ -23,9 +23,7 @@ P = 128
 PACK = 4
 HALF = S // 2
 BANKS = 8
-RANGES = ((0, P), (P, HALF), (HALF, S))
-W2_LATE = 4
-W2_GPSIMD = 3 * P // 2
+RANGES = 4
 WARM = 8
 
 
@@ -39,6 +37,7 @@ def tile_picked_modtrue_gelu_p_kernel(tc, x_words, x_scales, w1, wt, w2, offs, t
     with ExitStack() as ctx:
         lists = ctx.enter_context(tc.tile_pool(name="lists", bufs=1))
         keep = ctx.enter_context(tc.tile_pool(name="keep", bufs=1))
+        tail = ctx.enter_context(tc.tile_pool(name="tail", bufs=1))
         spare = ctx.enter_context(tc.tile_pool(name="spare", bufs=1))
         psum = ctx.enter_context(tc.psum_pool(name="psum", bufs=BANKS))
 
@@ -102,7 +101,7 @@ def tile_picked_modtrue_gelu_p_kernel(tc, x_words, x_scales, w1, wt, w2, offs, t
         by_vector(odd_cols[:, :, 1, 3], w1_cols[:, 1, :, 1, 3])
         quantize_w1(1, odd, 1, 0, P)
         warm_gelu = spare.tile([P, 1], F32, name="warm_gelu")
-        nc.scalar.activation(warm_gelu[:], w1_raw[:, 0, 0:1], GELU)
+        nc.scalar.activation(warm_gelu[:], warm_in[:, 0, 0:1], GELU)
         even = keep.tile([P, 2, P, PACK], BF16, name="w1_even", align_bytes=64)
         for a, b in ((0, 2), (2, 4)):
             by_scalar(even[:].rearrange("p u m j -> p m u j")[:, :, :, a:b], w1_cols[:, 0, :, :, a:b])
@@ -135,111 +134,104 @@ def tile_picked_modtrue_gelu_p_kernel(tc, x_words, x_scales, w1, wt, w2, offs, t
         window = {}
         for u in range(2):
             window[2 * u] = pairs[u][:].rearrange("p s c -> p (s c)")
-            window[2 * u + 1] = keep.tile([P, S], F32, name=f"single{u}", tag=f"single_then_z_{u}", align_bytes=64)[:]
+            window[2 * u + 1] = keep.tile([P, S], F32, name=f"single{u}", align_bytes=64)[:]
 
-        def fill_window(t, copy=by_scalar, parts=slice(None)):
-            for values, tokens in y[t][parts]:
+        def fill_window(t, copy):
+            for values, tokens in y[t]:
                 copy(window[t][:, tokens], values)
 
-        def activate_all(t):
+        def activate(t):
             done = keep.tile([P, S], F32, name=f"activated{t}", tag=f"activated_then_w2_{t}", align_bytes=64)
             for values, tokens in y[t]:
                 nc.scalar.activation(done[:, tokens], values, GELU)
             return done
 
-        def fetch_weighted(t, activated):
-            got = keep.tile([P, V], F32, name=f"weighted{t}")
-            nc.vector.tensor_tensor(got[:], activated[:].indirect(take_sb[:]), wt_sb[:], MULT)
+        def fetch_weighted(t, activated, got=None):
+            if got is None:
+                got = keep.tile([P, V], F32, name=f"weighted{t}", tag=f"weighted{t}_then_w2", align_bytes=64)[:]
+            nc.vector.tensor_tensor(got, activated[:].indirect(take_sb[:]), wt_sb[:], MULT)
             return got
 
-        def fetch_raw(t):
-            got = keep.tile([P, V], F32, name=f"raw{t}", tag=f"raw_then_w2_{t}", align_bytes=64)
-            nc.scalar.activation(got[:], window[t].indirect(take_sb[:]), COPY)
-            return got
+        def scatter_by_vector(t, values):
+            by_vector(window[t].indirect(take_sb[:]), values)
 
-        def activate(t, raw):
-            done = keep.tile([P, V], F32, name=f"activated{t}")
-            nc.scalar.activation(done[:], raw[:], GELU)
-            return done
+        def scatter_by_scalar(t, values):
+            nc.scalar.activation(window[t].indirect(take_sb[:]), values, COPY)
 
-        def scatter(t, values):
-            by_vector(window[t].indirect(take_sb[:]), values[:])
+        def group_w2(h, after):
+            grouped = keep.tile([P, HALF, PACK], BF16, name=f"w2_grouped{h}", tag=f"activated_then_w2_{after}", align_bytes=64)
+            group_by_gpsimd(grouped[:], w2_raw[:, :, h * HALF : (h + 1) * HALF])
+            return grouped
 
-        def scatter_weighted(t, values):
-            nc.vector.tensor_tensor(window[t].indirect(take_sb[:]), values[:], wt_sb[:], MULT)
+        slot = P * PACK * 2
+        z_grouped = {}
 
-        def group_w2(a, b):
-            by_scalar(
-                w2_grouped[a // HALF][:, a % HALF : a % HALF + b - a, :].rearrange("p (c i) j -> p c j i", i=4),
-                w2_raw[:, :, a:b].rearrange("p j (c i) -> p c j i", i=4),
-            )
+        def group_z(copy, u, r):
+            if r not in z_grouped:
+                z_grouped[r] = tail.tile([P, P, PACK], BF16, name=f"z_grouped{r}", offset=(0, 1, 2, 1)[r] * slot, align_bytes=64)
+            copy(z_grouped[r][:, :, 2 * u : 2 * u + 2], pairs[u][:, :, r * P : (r + 1) * P].rearrange("p s c -> p c s"))
 
-        def z_grouped(a, b):
-            return z_first[:, a:b, :] if b <= P else z_rest[:, a - P : b - P, :]
-
-        def group_z(copy, u, a, b):
-            copy(z_grouped(a, b)[:, :, 2 * u : 2 * u + 2], pairs[u][:, :, a:b].rearrange("p s c -> p c s"))
-
-        activated1 = activate_all(1)
-        fill_window(1, by_vector, slice(0, 3))
-        weighted1 = fetch_weighted(1, activated1)
-        activated3 = activate_all(3)
-        weighted3 = fetch_weighted(3, activated3)
-        fill_window(1, by_scalar, slice(3, 4))
-        scatter(1, weighted1)
-        w2_grouped = [keep.tile([P, HALF, PACK], BF16, name="w2_grouped0", tag="activated_then_w2_3", align_bytes=64)]
-        group_by_gpsimd(w2_grouped[0][:, 0:W2_GPSIMD, :], w2_raw[:, :, 0:W2_GPSIMD])
-        fill_window(0)
-        fill_window(3)
-        scatter(3, weighted3)
-        raw0 = fetch_raw(0)
-        fill_window(2)
-        activated0 = activate(0, raw0)
-        nc.gpsimd.tensor_scalar(pairs[0][:, 1, :], window[1], 1.0, 0.0, MULT, ADD)
-        scatter_weighted(0, activated0)
-        raw2 = fetch_raw(2)
-        group_w2(W2_GPSIMD, HALF)
-        activated2 = activate(2, raw2)
-        by_scalar(pairs[1][:, 1, :], window[3])
-        w2_grouped.append(keep.tile([P, HALF, PACK], BF16, name="w2_grouped1", tag="raw_then_w2_2", align_bytes=64))
-        group_w2(HALF, N - W2_LATE)
-        scatter_weighted(2, activated2)
-        z_first = keep.tile([P, P, PACK], BF16, name="z_first", tag="single_then_z_1", align_bytes=64)
-        z_rest = keep.tile([P, S - P, PACK], BF16, name="z_rest", align_bytes=64)
-        group_z(by_vector, 0, 0, P)
-        group_z(by_scalar, 0, P, S)
-
-        w2_codes = keep.tile([P, N], U32, name="w2_codes", tag="scales_wt_w2", align_bytes=64)
-        w2_scale = keep.tile([P, N], U8, name="w2_scale", align_bytes=64)
         z_codes = keep.tile([P, S], U32, name="z_codes", align_bytes=64)
         z_scale = keep.tile([P, S], U8, name="z_scale", align_bytes=64)
 
         def quantize_w2(h):
-            cols = slice(h * HALF, (h + 1) * HALF)
+            if h == 0:
+                codes = keep.tile([P, HALF], U32, name="w2_codes0", tag="weighted0_then_w2", align_bytes=64)
+            else:
+                codes = tail.tile([P, HALF], U32, name="w2_codes1", offset=0, align_bytes=64)
+            w2_codes.append(codes)
             nc.vector.quantize_mx(
-                w2_codes[:, cols].bitcast(FP8X4), w2_scale[:, cols], w2_grouped[h][:].rearrange("p c j -> p (c j)")
+                codes[:].bitcast(FP8X4), w2_scale[:, h * HALF : (h + 1) * HALF], w2_grouped[h][:].rearrange("p c j -> p (c j)")
             )
 
         def quantize_z(r):
-            a, b = RANGES[r]
-            nc.vector.quantize_mx(z_codes[:, a:b].bitcast(FP8X4), z_scale[:, a:b], z_grouped(a, b).rearrange("p c j -> p (c j)"))
+            a, b = r * P, (r + 1) * P
+            nc.vector.quantize_mx(z_codes[:, a:b].bitcast(FP8X4), z_scale[:, a:b], z_grouped[r][:].rearrange("p c j -> p (c j)"))
 
-        group_z(by_vector, 1, *RANGES[0])
-        group_z(by_scalar, 1, *RANGES[1])
-        group_w2(N - W2_LATE, N)
-        group_z(by_scalar, 1, *RANGES[2])
+        activated1 = activate(1)
+        fill_window(1, by_vector)
+        weighted1 = fetch_weighted(1, activated1)
+        activated3 = activate(3)
+        weighted3 = fetch_weighted(3, activated3)
+        fill_window(3, by_scalar)
+        scatter_by_vector(1, weighted1)
+        w2_grouped = [group_w2(0, 3)]
+        activated0 = activate(0)
+        activated2 = activate(2)
+        scatter_by_scalar(3, weighted3)
+        fill_window(0, by_vector)
+        nc.gpsimd.tensor_scalar(pairs[0][:, 1, :], window[1], 1.0, 0.0, MULT, ADD)
+        weighted0 = fetch_weighted(0, activated0)
+        last = tail.tile([P, V + 32], F32, name="weighted2", offset=slot - 64, align_bytes=64)
+        weighted2 = fetch_weighted(2, activated2, last[:, 0:V])
+        fill_window(2, by_scalar)
+        by_scalar(pairs[1][:, 1, :], window[3])
+        scatter_by_scalar(2, weighted2)
+        w2_grouped.append(group_w2(1, 2))
+        scatter_by_vector(0, weighted0)
+        w2_codes = []
+        w2_scale = keep.tile([P, N], U8, name="w2_scale", align_bytes=64)
         quantize_w2(0)
+
+        for r in range(2):
+            group_z(by_vector, 0, r)
+            group_z(by_scalar, 1, r)
         quantize_z(0)
         quantize_z(1)
         quantize_w2(1)
+        group_z(by_scalar, 1, 2)
+        group_z(by_vector, 0, 2)
+        group_z(by_vector, 0, 3)
+        group_z(by_vector, 1, 3)
         quantize_z(2)
+        quantize_z(3)
 
         out_rows = out.rearrange("(mt p) j -> p mt j", p=P)
 
         def second_product(mt, a, b, dest):
             nc.tensor.matmul_mx(
                 dest,
-                lhsT=w2_codes[:, mt * P : (mt + 1) * P].bitcast(FP8X4),
+                lhsT=w2_codes[mt // 2][:, mt % 2 * P : (mt % 2 + 1) * P].bitcast(FP8X4),
                 lhsT_scale=w2_scale[:, mt * P : (mt + 1) * P],
                 rhs=z_codes[:, a:b].bitcast(FP8X4),
                 rhs_scale=z_scale[:, a:b],
@@ -257,12 +249,12 @@ def tile_picked_modtrue_gelu_p_kernel(tc, x_words, x_scales, w1, wt, w2, offs, t
 
         result(0, (0, P), by_scalar)
         result(0, (P, HALF), by_scalar)
-        result(1, (0, HALF), by_vector)
+        result(1, (0, P, HALF), by_scalar)
         result(2, (0, HALF), by_scalar)
-        result(3, (0, HALF), by_vector)
-        result(0, (HALF, S), by_scalar)
-        result(1, (HALF, S), by_vector)
-        result(2, (HALF, S), by_scalar)
+        result(3, (0, HALF), by_scalar)
+        result(0, (HALF, HALF + P, S), by_vector)
+        result(1, (HALF, S), by_scalar)
+        result(2, (HALF, S), by_vector)
         staged = keep.tile([P, HALF], F32, name="staged_last")
         for i, copy in enumerate((by_vector, by_scalar)):
             bank = new_bank()

@@ -47,7 +47,7 @@ def tile_picked_modtrue_gelu_p_kernel(tc, x_words, x_scales, w1, wt, w2, offs, t
 
         scale_table = keep.tile([P, T], U8, name="scale_table", tag="scales_wt_w2", align_bytes=64)
         for a, b in ((0, 48), (64, P)):
-            nc.vector.memset(scale_table[a:b, :].bitcast(I32), 0)
+            nc.gpsimd.memset(scale_table[a:b, :].bitcast(I32), 0)
         x_scale = keep.tile([P, S], U8, name="x_scale", align_bytes=64)
         nc.vector.memset(x_scale[:].bitcast(I32), 0)
         nc.scalar.dma_start(scale_table[48:64, :].bitcast(I32), x_scales[0].bitcast(I32))
@@ -93,28 +93,24 @@ def tile_picked_modtrue_gelu_p_kernel(tc, x_words, x_scales, w1, wt, w2, offs, t
         odd_cols = odd[:].rearrange("p u m j -> p m u j")
         by_vector(odd_cols[:, :, :, 0:2], w1_cols[:, 1, :, :, 0:2])
         by_vector(odd_cols[:, :, :, 2], w1_cols[:, 1, :, :, 2])
-        column_halves = ((0, P // 2), (P // 2, P))
-        for a, b in column_halves:
-            by_vector(odd_cols[:, a:b, 0, 3], w1_cols[:, 1, a:b, 0, 3])
-        for a, b in column_halves:
-            quantize_w1(1, odd, 0, a, b)
+        by_vector(odd_cols[:, :, 0, 3], w1_cols[:, 1, :, 0, 3])
         by_vector(odd_cols[:, :, 1, 3], w1_cols[:, 1, :, 1, 3])
-        quantize_w1(1, odd, 1, 0, P)
+        for u in range(2):
+            quantize_w1(1, odd, u, 0, P)
         warm_gelu = spare.tile([P, 1], F32, name="warm_gelu")
         nc.scalar.activation(warm_gelu[:], warm_in[:, 0, 0:1], GELU)
         even = keep.tile([P, 2, P, PACK], BF16, name="w1_even", align_bytes=64)
         for a, b in ((0, 2), (2, 4)):
             by_scalar(even[:].rearrange("p u m j -> p m u j")[:, :, :, a:b], w1_cols[:, 0, :, :, a:b])
-        for u in range(2):
-            quantize_w1(0, even, u, 0, P)
+        nc.vector.quantize_mx(w1_codes[0][:].bitcast(FP8X4), w1_scale[0][:], even[:].rearrange("p u m j -> p (u m j)"))
 
         def new_bank():
             return psum.tile([P, S], F32, name="bank")
 
-        def first_product(t, parts):
-            at, width, made = (t // 2) * P, S // parts, []
-            for a in range(0, S, width):
-                tokens = slice(a, a + width)
+        def first_product(t, cuts):
+            at, made = (t // 2) * P, []
+            for a, b in zip(cuts, cuts[1:]):
+                tokens, width = slice(a, b), b - a
                 values = new_bank()[:, 0:width]
                 nc.tensor.matmul_mx(
                     values,
@@ -128,7 +124,7 @@ def tile_picked_modtrue_gelu_p_kernel(tc, x_words, x_scales, w1, wt, w2, offs, t
                 made.append((values, tokens))
             return made
 
-        y = {t: first_product(t, parts) for t, parts in ((1, 4), (3, 2), (0, 1), (2, 1))}
+        y = {t: first_product(t, cuts) for t, cuts in ((1, (0, P, HALF, HALF + P, S)), (3, (0, HALF, S)), (0, (0, S)), (2, (0, S)))}
 
         pairs = [keep.tile([P, 2, S], F32, name=f"pair{u}") for u in range(2)]
         window = {}
@@ -136,8 +132,8 @@ def tile_picked_modtrue_gelu_p_kernel(tc, x_words, x_scales, w1, wt, w2, offs, t
             window[2 * u] = pairs[u][:].rearrange("p s c -> p (s c)")
             window[2 * u + 1] = keep.tile([P, S], F32, name=f"single{u}", align_bytes=64)[:]
 
-        def fill_window(t, copy):
-            for values, tokens in y[t]:
+        def fill_window(t, copy, parts=slice(None)):
+            for values, tokens in y[t][parts]:
                 copy(window[t][:, tokens], values)
 
         def activate(t):
@@ -189,10 +185,11 @@ def tile_picked_modtrue_gelu_p_kernel(tc, x_words, x_scales, w1, wt, w2, offs, t
             nc.vector.quantize_mx(z_codes[:, a:b].bitcast(FP8X4), z_scale[:, a:b], z_grouped[r][:].rearrange("p c j -> p (c j)"))
 
         activated1 = activate(1)
-        fill_window(1, by_vector)
+        fill_window(1, by_vector, slice(0, 3))
         weighted1 = fetch_weighted(1, activated1)
         activated3 = activate(3)
         weighted3 = fetch_weighted(3, activated3)
+        fill_window(1, by_scalar, slice(3, 4))
         fill_window(3, by_scalar)
         scatter_by_vector(1, weighted1)
         w2_grouped = [group_w2(0, 3)]
@@ -200,7 +197,7 @@ def tile_picked_modtrue_gelu_p_kernel(tc, x_words, x_scales, w1, wt, w2, offs, t
         activated2 = activate(2)
         scatter_by_scalar(3, weighted3)
         fill_window(0, by_vector)
-        nc.gpsimd.tensor_scalar(pairs[0][:, 1, :], window[1], 1.0, 0.0, MULT, ADD)
+        by_vector(pairs[0][:, 1, :], window[1])
         weighted0 = fetch_weighted(0, activated0)
         last = tail.tile([P, V + 32], F32, name="weighted2", offset=slot - 64, align_bytes=64)
         weighted2 = fetch_weighted(2, activated2, last[:, 0:V])
@@ -255,9 +252,4 @@ def tile_picked_modtrue_gelu_p_kernel(tc, x_words, x_scales, w1, wt, w2, offs, t
         result(0, (HALF, HALF + P, S), by_vector)
         result(1, (HALF, S), by_scalar)
         result(2, (HALF, S), by_vector)
-        staged = keep.tile([P, HALF], F32, name="staged_last")
-        for i, copy in enumerate((by_vector, by_scalar)):
-            bank = new_bank()
-            second_product(3, HALF + i * P, HALF + (i + 1) * P, bank[:, 0:P])
-            copy(staged[:, i * P : (i + 1) * P], bank[:, 0:P])
-        nc.sync.dma_start(out_rows[:, 3, HALF:S], staged[:])
+        result(3, (HALF, S), by_scalar)

@@ -189,16 +189,16 @@ def tile_picked_modtrue_gelu_p_kernel(tc, x_words, x_scales, w1, wt, w2, offs, t
         weighted1 = fetch_weighted(1, activated1)
         activated3 = activate(3)
         weighted3 = fetch_weighted(3, activated3)
+        activated0 = activate(0)
+        weighted0 = fetch_weighted(0, activated0)
         fill_window(1, by_scalar, slice(3, 4))
         fill_window(3, by_scalar)
         scatter_by_vector(1, weighted1)
-        w2_grouped = [group_w2(0, 3)]
-        activated0 = activate(0)
-        activated2 = activate(2)
-        scatter_by_scalar(3, weighted3)
+        w2_grouped = [group_w2(0, 0)]
         fill_window(0, by_vector)
         by_vector(pairs[0][:, 1, :], window[1])
-        weighted0 = fetch_weighted(0, activated0)
+        activated2 = activate(2)
+        scatter_by_scalar(3, weighted3)
         last = tail.tile([P, V + 32], F32, name="weighted2", offset=slot - 64, align_bytes=64)
         weighted2 = fetch_weighted(2, activated2, last[:, 0:V])
         fill_window(2, by_scalar)

@@ -199,8 +199,8 @@ def tile_picked_modtrue_gelu_p_kernel(tc, x_words, x_scales, w1, wt, w2, offs, t
         by_vector(pairs[0][:, 1, :], window[1])
         activated2 = activate(2)
         scatter_by_scalar(3, weighted3)
-        last = tail.tile([P, V + 32], F32, name="weighted2", offset=slot - 64, align_bytes=64)
-        weighted2 = fetch_weighted(2, activated2, last[:, 0:V])
+        last = tail.tile([P, V], F32, name="weighted2", offset=3 * slot // 2, align_bytes=64)
+        weighted2 = fetch_weighted(2, activated2, last[:])
         fill_window(2, by_scalar)
         by_scalar(pairs[1][:, 1, :], window[3])
         scatter_by_scalar(2, weighted2)
@@ -210,16 +210,17 @@ def tile_picked_modtrue_gelu_p_kernel(tc, x_words, x_scales, w1, wt, w2, offs, t
         w2_scale = keep.tile([P, N], U8, name="w2_scale", align_bytes=64)
         quantize_w2(0)
 
-        for r in range(2):
-            group_z(by_vector, 0, r)
+        group_z(by_vector, 0, 0)
+        group_z(by_vector, 1, 0)
+        group_z(by_vector, 0, 1)
+        for r in (1, 2):
             group_z(by_scalar, 1, r)
         quantize_z(0)
         quantize_z(1)
         quantize_w2(1)
-        group_z(by_scalar, 1, 2)
+        group_z(by_scalar, 1, 3)
         group_z(by_vector, 0, 2)
         group_z(by_vector, 0, 3)
-        group_z(by_vector, 1, 3)
         quantize_z(2)
         quantize_z(3)
 

@@ -54,9 +54,7 @@ def tile_picked_modtrue_gelu_p_kernel(tc, x_words, x_scales, w1, wt, w2, offs, t
         nc.sync.dma_start(offs_sb[:], offs)
 
         warm_in = spare.tile([P, PACK, WARM], F32, name="warm_in")
-        warm_out = spare.tile([P, WARM, PACK], BF16, name="warm_out")
         nc.gpsimd.memset(warm_in[:], 0.0)
-        group_by_gpsimd(warm_out[:], warm_in[:])
 
         word_table = keep.tile([P, T], U32, name="word_table", tag="words_then_w2", align_bytes=64)
         nc.sync.dma_start(word_table[:].bitcast(I32), x_words[0].rearrange("p n r -> p (n r)").bitcast(I32))

@@ -23,21 +23,33 @@ P = 128
 PACK = 4
 HALF = S // 2
 BANKS = 8
-RANGES = 4
-WARM = 8
+BLOCKS = K // 32
+SCALE_AT = 64 - BLOCKS
+SLOT = P * PACK * 2
 
 
 def tile_picked_modtrue_gelu_p_kernel(tc, x_words, x_scales, w1, wt, w2, offs, take, out):
     nc = tc.nc
     by_vector, by_scalar = nc.vector.tensor_copy, nc.scalar.copy
 
-    def group_by_gpsimd(grouped, rows):
-        nc.gpsimd.tensor_scalar(grouped, rows.rearrange("p j c -> p c j"), 1.0, 0.0, MULT, ADD)
+    def quantize(codes, scale, grouped):
+        nc.vector.quantize_mx(codes.bitcast(FP8X4), scale, grouped.rearrange("p c j -> p (c j)"))
+
+    def multiply(dest, weights, weights_scale, moving, moving_scale):
+        nc.tensor.matmul_mx(
+            dest,
+            lhsT=weights.bitcast(FP8X4),
+            lhsT_scale=weights_scale,
+            rhs=moving.bitcast(FP8X4),
+            rhs_scale=moving_scale,
+            start=True,
+            stop=True,
+        )
 
     with ExitStack() as ctx:
         lists = ctx.enter_context(tc.tile_pool(name="lists", bufs=1))
         keep = ctx.enter_context(tc.tile_pool(name="keep", bufs=1))
-        tail = ctx.enter_context(tc.tile_pool(name="tail", bufs=1))
+        placed = ctx.enter_context(tc.tile_pool(name="placed", bufs=1))
         spare = ctx.enter_context(tc.tile_pool(name="spare", bufs=1))
         psum = ctx.enter_context(tc.psum_pool(name="psum", bufs=BANKS))
 
@@ -45,15 +57,15 @@ def tile_picked_modtrue_gelu_p_kernel(tc, x_words, x_scales, w1, wt, w2, offs, t
         offs_sb = lists.tile([P, S // 16], U16, name="offs_sb")
         take_sb = lists.tile([P, V // 16], U16, name="take_sb")
 
-        scale_table = keep.tile([P, T], U8, name="scale_table", tag="scales_wt_w2", align_bytes=64)
-        for a, b in ((0, 48), (64, P)):
+        scale_table = keep.tile([P, T], U8, name="scale_table", tag="scales_then_wt", align_bytes=64)
+        for a, b in ((0, SCALE_AT), (SCALE_AT + BLOCKS, P)):
             nc.gpsimd.memset(scale_table[a:b, :].bitcast(I32), 0)
         x_scale = keep.tile([P, S], U8, name="x_scale", align_bytes=64)
         nc.vector.memset(x_scale[:].bitcast(I32), 0)
-        nc.scalar.dma_start(scale_table[48:64, :].bitcast(I32), x_scales[0].bitcast(I32))
+        nc.scalar.dma_start(scale_table[SCALE_AT : SCALE_AT + BLOCKS, :].bitcast(I32), x_scales[0].bitcast(I32))
         nc.sync.dma_start(offs_sb[:], offs)
 
-        warm_in = spare.tile([P, PACK, WARM], F32, name="warm_in")
+        warm_in = spare.tile([P, 1], F32, name="warm_in")
         nc.gpsimd.memset(warm_in[:], 0.0)
 
         word_table = keep.tile([P, T], U32, name="word_table", tag="words_then_w2", align_bytes=64)
@@ -67,8 +79,9 @@ def tile_picked_modtrue_gelu_p_kernel(tc, x_words, x_scales, w1, wt, w2, offs, t
         picked_scale = keep.tile([P, S], U8, name="picked_scale", align_bytes=64)
         by_vector(picked_scale[:], scale_table[:].indirect(offs_sb[:]))
         for q in range(4):
-            nc.scalar.dma_start(x_scale[32 * q : 32 * q + 4, :].bitcast(I32), picked_scale[48 + 4 * q : 52 + 4 * q, :].bitcast(I32))
-        wt_sb = keep.tile([P, V], F32, name="wt_sb", tag="scales_wt_w2", align_bytes=64)
+            rows = slice(SCALE_AT + 4 * q, SCALE_AT + 4 * q + 4)
+            nc.scalar.dma_start(x_scale[32 * q : 32 * q + 4, :].bitcast(I32), picked_scale[rows, :].bitcast(I32))
+        wt_sb = keep.tile([P, V], F32, name="wt_sb", tag="scales_then_wt", align_bytes=64)
         nc.sync.dma_start(wt_sb[:], wt.rearrange("(p j) v -> p j v", j=PACK)[:, 0, :])
 
         x_codes = keep.tile([P, S], U32, name="x_codes", align_bytes=64)
@@ -81,167 +94,139 @@ def tile_picked_modtrue_gelu_p_kernel(tc, x_words, x_scales, w1, wt, w2, offs, t
         w1_codes = {e: keep.tile([P, H // 2], U32, name=f"w1_codes{e}", align_bytes=64) for e in (1, 0)}
         w1_scale = {e: keep.tile([P, H // 2], U8, name=f"w1_scale{e}", align_bytes=64) for e in (1, 0)}
 
-        def quantize_w1(e, grouped, u, a, b):
-            cols = slice(u * P + a, u * P + b)
-            nc.vector.quantize_mx(
-                w1_codes[e][:, cols].bitcast(FP8X4), w1_scale[e][:, cols], grouped[:, u, a:b, :].rearrange("p m j -> p (m j)")
-            )
-
-        odd = keep.tile([P, 2, P, PACK], BF16, name="w1_odd", tag="w1_grouped", align_bytes=64)
+        odd = keep.tile([P, 2, P, PACK], BF16, name="w1_odd", align_bytes=64)
         odd_cols = odd[:].rearrange("p u m j -> p m u j")
         by_vector(odd_cols[:, :, :, 0:2], w1_cols[:, 1, :, :, 0:2])
         by_vector(odd_cols[:, :, :, 2], w1_cols[:, 1, :, :, 2])
-        by_vector(odd_cols[:, :, 0, 3], w1_cols[:, 1, :, 0, 3])
-        by_vector(odd_cols[:, :, 1, 3], w1_cols[:, 1, :, 1, 3])
         for u in range(2):
-            quantize_w1(1, odd, u, 0, P)
+            by_vector(odd_cols[:, :, u, 3], w1_cols[:, 1, :, u, 3])
+        for u in range(2):
+            quantize(w1_codes[1][:, u * P : (u + 1) * P], w1_scale[1][:, u * P : (u + 1) * P], odd[:, u, :, :])
+
         warm_gelu = spare.tile([P, 1], F32, name="warm_gelu")
-        nc.scalar.activation(warm_gelu[:], warm_in[:, 0, 0:1], GELU)
+        nc.scalar.activation(warm_gelu[:], warm_in[:], GELU)
+
         even = keep.tile([P, 2, P, PACK], BF16, name="w1_even", align_bytes=64)
         for a, b in ((0, 2), (2, 4)):
             by_scalar(even[:].rearrange("p u m j -> p m u j")[:, :, :, a:b], w1_cols[:, 0, :, :, a:b])
-        nc.vector.quantize_mx(w1_codes[0][:].bitcast(FP8X4), w1_scale[0][:], even[:].rearrange("p u m j -> p (u m j)"))
+        quantize(w1_codes[0][:], w1_scale[0][:], even[:].rearrange("p u m j -> p (u m) j"))
 
         def new_bank():
             return psum.tile([P, S], F32, name="bank")
 
-        def first_product(t, cuts):
-            at, made = (t // 2) * P, []
-            for a, b in zip(cuts, cuts[1:]):
-                tokens, width = slice(a, b), b - a
+        def first_product(t, parts):
+            cols, width, made = slice((t // 2) * P, (t // 2 + 1) * P), S // parts, []
+            for a in range(0, S, width):
+                tokens = slice(a, a + width)
                 values = new_bank()[:, 0:width]
-                nc.tensor.matmul_mx(
-                    values,
-                    lhsT=w1_codes[t % 2][:, at : at + P].bitcast(FP8X4),
-                    lhsT_scale=w1_scale[t % 2][:, at : at + P],
-                    rhs=x_codes[:, tokens].bitcast(FP8X4),
-                    rhs_scale=x_scale[:, tokens],
-                    start=True,
-                    stop=True,
-                )
+                multiply(values, w1_codes[t % 2][:, cols], w1_scale[t % 2][:, cols], x_codes[:, tokens], x_scale[:, tokens])
                 made.append((values, tokens))
             return made
 
-        y = {t: first_product(t, cuts) for t, cuts in ((1, (0, P, HALF, HALF + P, S)), (3, (0, HALF, S)), (0, (0, S)), (2, (0, S)))}
+        y = {t: first_product(t, parts) for t, parts in ((1, 4), (3, 2), (0, 1), (2, 1))}
 
         pairs = [keep.tile([P, 2, S], F32, name=f"pair{u}") for u in range(2)]
         window = {}
         for u in range(2):
             window[2 * u] = pairs[u][:].rearrange("p s c -> p (s c)")
             window[2 * u + 1] = keep.tile([P, S], F32, name=f"single{u}", align_bytes=64)[:]
+        z_codes = keep.tile([P, S], U32, name="z_codes", align_bytes=64)
+        z_scale = keep.tile([P, S], U8, name="z_scale", align_bytes=64)
 
         def fill_window(t, copy, parts=slice(None)):
             for values, tokens in y[t][parts]:
                 copy(window[t][:, tokens], values)
 
         def activate(t):
-            done = keep.tile([P, S], F32, name=f"activated{t}", tag=f"activated_then_w2_{t}", align_bytes=64)
+            done = keep.tile([P, S], F32, name=f"activated{t}", align_bytes=64)
             for values, tokens in y[t]:
                 nc.scalar.activation(done[:, tokens], values, GELU)
             return done
 
-        def fetch_weighted(t, activated, got=None):
-            if got is None:
-                got = keep.tile([P, V], F32, name=f"weighted{t}", tag=f"weighted{t}_then_w2", align_bytes=64)[:]
-            nc.vector.tensor_tensor(got, activated[:].indirect(take_sb[:]), wt_sb[:], MULT)
+        def fetch_weighted(t, activated, pool, **place):
+            got = pool.tile([P, V], F32, name=f"weighted{t}", align_bytes=64, **place)
+            nc.vector.tensor_tensor(got[:], activated[:].indirect(take_sb[:]), wt_sb[:], MULT)
             return got
 
         def scatter_by_vector(t, values):
-            by_vector(window[t].indirect(take_sb[:]), values)
+            by_vector(window[t].indirect(take_sb[:]), values[:])
 
         def scatter_by_scalar(t, values):
-            nc.scalar.activation(window[t].indirect(take_sb[:]), values, COPY)
+            nc.scalar.activation(window[t].indirect(take_sb[:]), values[:], COPY)
 
-        def group_w2(h, after):
-            grouped = keep.tile([P, HALF, PACK], BF16, name=f"w2_grouped{h}", tag=f"activated_then_w2_{after}", align_bytes=64)
-            group_by_gpsimd(grouped[:], w2_raw[:, :, h * HALF : (h + 1) * HALF])
+        def group_w2(h, behind):
+            grouped = keep.tile([P, HALF, PACK], BF16, name=f"w2_grouped{h}", tag=behind, align_bytes=64)
+            rows = w2_raw[:, :, h * HALF : (h + 1) * HALF]
+            nc.gpsimd.tensor_scalar(grouped[:], rows.rearrange("p j c -> p c j"), 1.0, 0.0, MULT, ADD)
             return grouped
-
-        slot = P * PACK * 2
-        z_grouped = {}
-
-        def group_z(copy, u, r):
-            if r not in z_grouped:
-                z_grouped[r] = tail.tile([P, P, PACK], BF16, name=f"z_grouped{r}", offset=(0, 1, 2, 1)[r] * slot, align_bytes=64)
-            copy(z_grouped[r][:, :, 2 * u : 2 * u + 2], pairs[u][:, :, r * P : (r + 1) * P].rearrange("p s c -> p c s"))
-
-        z_codes = keep.tile([P, S], U32, name="z_codes", align_bytes=64)
-        z_scale = keep.tile([P, S], U8, name="z_scale", align_bytes=64)
-
-        def quantize_w2(h):
-            if h == 0:
-                codes = keep.tile([P, HALF], U32, name="w2_codes0", tag="weighted0_then_w2", align_bytes=64)
-            else:
-                codes = tail.tile([P, HALF], U32, name="w2_codes1", offset=0, align_bytes=64)
-            w2_codes.append(codes)
-            nc.vector.quantize_mx(
-                codes[:].bitcast(FP8X4), w2_scale[:, h * HALF : (h + 1) * HALF], w2_grouped[h][:].rearrange("p c j -> p (c j)")
-            )
-
-        def quantize_z(r):
-            a, b = r * P, (r + 1) * P
-            nc.vector.quantize_mx(z_codes[:, a:b].bitcast(FP8X4), z_scale[:, a:b], z_grouped[r][:].rearrange("p c j -> p (c j)"))
 
         activated1 = activate(1)
         fill_window(1, by_vector, slice(0, 3))
-        weighted1 = fetch_weighted(1, activated1)
-        activated3 = activate(3)
-        weighted3 = fetch_weighted(3, activated3)
-        activated0 = activate(0)
-        weighted0 = fetch_weighted(0, activated0)
+        weighted1 = fetch_weighted(1, activated1, keep)
+        weighted3 = fetch_weighted(3, activate(3), keep)
+        weighted0 = fetch_weighted(0, activate(0), keep)
         fill_window(1, by_scalar, slice(3, 4))
         fill_window(3, by_scalar)
+
         scatter_by_vector(1, weighted1)
-        w2_grouped = [group_w2(0, 0)]
+        w2_grouped = [group_w2(0, "activated0")]
         fill_window(0, by_vector)
         by_vector(pairs[0][:, 1, :], window[1])
         activated2 = activate(2)
         scatter_by_scalar(3, weighted3)
-        last = tail.tile([P, V], F32, name="weighted2", offset=3 * slot // 2, align_bytes=64)
-        weighted2 = fetch_weighted(2, activated2, last[:])
+
+        weighted2 = fetch_weighted(2, activated2, placed, offset=3 * SLOT // 2)
         fill_window(2, by_scalar)
         by_scalar(pairs[1][:, 1, :], window[3])
         scatter_by_scalar(2, weighted2)
-        w2_grouped.append(group_w2(1, 2))
+        w2_grouped.append(group_w2(1, "activated2"))
         scatter_by_vector(0, weighted0)
-        w2_codes = []
-        w2_scale = keep.tile([P, N], U8, name="w2_scale", align_bytes=64)
-        quantize_w2(0)
 
+        w2_scale = keep.tile([P, N], U8, name="w2_scale", align_bytes=64)
+        w2_codes, z_grouped = [], {}
+
+        def quantize_w2(h, pool, **place):
+            w2_codes.append(pool.tile([P, HALF], U32, name=f"w2_codes{h}", align_bytes=64, **place))
+            quantize(w2_codes[h][:], w2_scale[:, h * HALF : (h + 1) * HALF], w2_grouped[h][:])
+
+        def new_range(r, slot):
+            z_grouped[r] = placed.tile([P, P, PACK], BF16, name=f"z_grouped{r}", offset=slot * SLOT, align_bytes=64)
+
+        def group_z(copy, u, r):
+            copy(z_grouped[r][:, :, 2 * u : 2 * u + 2], pairs[u][:, :, r * P : (r + 1) * P].rearrange("p s c -> p c s"))
+
+        def quantize_z(r):
+            quantize(z_codes[:, r * P : (r + 1) * P], z_scale[:, r * P : (r + 1) * P], z_grouped[r][:])
+
+        quantize_w2(0, keep, tag="weighted0")
+        new_range(0, 0)
         group_z(by_vector, 0, 0)
         group_z(by_vector, 1, 0)
+        new_range(1, 1)
         group_z(by_vector, 0, 1)
-        for r in (1, 2):
-            group_z(by_scalar, 1, r)
+        group_z(by_scalar, 1, 1)
+        new_range(2, 2)
+        group_z(by_scalar, 0, 2)
+        group_z(by_scalar, 1, 2)
         quantize_z(0)
         quantize_z(1)
-        quantize_w2(1)
-        group_z(by_scalar, 1, 3)
-        group_z(by_vector, 0, 2)
+        quantize_w2(1, placed, offset=0)
+        new_range(3, 1)
         group_z(by_vector, 0, 3)
+        group_z(by_vector, 1, 3)
         quantize_z(2)
         quantize_z(3)
 
         out_rows = out.rearrange("(mt p) j -> p mt j", p=P)
 
-        def second_product(mt, a, b, dest):
-            nc.tensor.matmul_mx(
-                dest,
-                lhsT=w2_codes[mt // 2][:, mt % 2 * P : (mt % 2 + 1) * P].bitcast(FP8X4),
-                lhsT_scale=w2_scale[:, mt * P : (mt + 1) * P],
-                rhs=z_codes[:, a:b].bitcast(FP8X4),
-                rhs_scale=z_scale[:, a:b],
-                start=True,
-                stop=True,
-            )
-
         def result(mt, cuts, copy):
-            bank = new_bank()
+            bank, first, width = new_bank(), cuts[0], cuts[-1] - cuts[0]
+            weights = w2_codes[mt // 2][:, mt % 2 * P : (mt % 2 + 1) * P]
             for a, b in zip(cuts, cuts[1:]):
-                second_product(mt, a, b, bank[:, a - cuts[0] : b - cuts[0]])
-            staged = keep.tile([P, cuts[-1] - cuts[0]], F32, name=f"staged{mt}_{cuts[0]}")
-            copy(staged[:], bank[:, 0 : cuts[-1] - cuts[0]])
-            nc.sync.dma_start(out_rows[:, mt, cuts[0] : cuts[-1]], staged[:])
+                multiply(bank[:, a - first : b - first], weights, w2_scale[:, mt * P : (mt + 1) * P], z_codes[:, a:b], z_scale[:, a:b])
+            staged = keep.tile([P, width], F32, name=f"staged{mt}_{first}")
+            copy(staged[:], bank[:, 0:width])
+            nc.sync.dma_start(out_rows[:, mt, first : first + width], staged[:])
 
         result(0, (0, P), by_scalar)
         result(0, (P, HALF), by_scalar)
@@ -251,4 +236,9 @@ def tile_picked_modtrue_gelu_p_kernel(tc, x_words, x_scales, w1, wt, w2, offs, t
         result(0, (HALF, HALF + P, S), by_vector)
         result(1, (HALF, S), by_scalar)
         result(2, (HALF, S), by_vector)
-        result(3, (HALF, S), by_scalar)
+        staged = keep.tile([P, HALF], F32, name="staged_last")
+        for i, copy in enumerate((by_vector, by_scalar)):
+            bank, tokens = new_bank(), slice(HALF + i * P, HALF + (i + 1) * P)
+            multiply(bank[:, 0:P], w2_codes[1][:, P:HALF], w2_scale[:, N - P : N], z_codes[:, tokens], z_scale[:, tokens])
+            copy(staged[:, i * P : (i + 1) * P], bank[:, 0:P])
+        nc.sync.dma_start(out_rows[:, 3, HALF:S], staged[:])

from contextlib import ExitStack

import concourse.mybir as mybir

K, T, S, V, N, H = 512, 2048, 512, 256, 512, 512

FLOPS = 2 * K * H * S + 2 * H * N * S
BYTES = K * T + K * T // 32 + 4 * (K * H + H * N + 8 * V + N * S) + 2 * 128 * (S + V) // 16

F32 = mybir.dt.float32
BF16 = mybir.dt.bfloat16
I32 = mybir.dt.int32
U32 = mybir.dt.uint32
U16 = mybir.dt.uint16
U8 = mybir.dt.uint8
FP8X4 = mybir.dt.float8_e4m3fn_x4
GELU = mybir.ActivationFunctionType.Gelu_apprx_tanh
COPY = mybir.ActivationFunctionType.Copy
MULT = mybir.AluOpType.mult
ADD = mybir.AluOpType.add

P = 128
PACK = 4
HALF = S // 2
BANKS = 8
BLOCKS = K // 32
SCALE_AT = 64 - BLOCKS
SLOT = P * PACK * 2


def tile_picked_modtrue_gelu_p_kernel(tc, x_words, x_scales, w1, wt, w2, offs, take, out):
    nc = tc.nc
    by_vector, by_scalar = nc.vector.tensor_copy, nc.scalar.copy

    def quantize(codes, scale, grouped):
        nc.vector.quantize_mx(codes.bitcast(FP8X4), scale, grouped.rearrange("p c j -> p (c j)"))

    def multiply(dest, weights, weights_scale, moving, moving_scale):
        nc.tensor.matmul_mx(
            dest,
            lhsT=weights.bitcast(FP8X4),
            lhsT_scale=weights_scale,
            rhs=moving.bitcast(FP8X4),
            rhs_scale=moving_scale,
            start=True,
            stop=True,
        )

    with ExitStack() as ctx:
        lists = ctx.enter_context(tc.tile_pool(name="lists", bufs=1))
        keep = ctx.enter_context(tc.tile_pool(name="keep", bufs=1))
        placed = ctx.enter_context(tc.tile_pool(name="placed", bufs=1))
        spare = ctx.enter_context(tc.tile_pool(name="spare", bufs=1))
        psum = ctx.enter_context(tc.psum_pool(name="psum", bufs=BANKS))


        offs_sb = lists.tile([P, S // 16], U16, name="offs_sb")
        take_sb = lists.tile([P, V // 16], U16, name="take_sb")

        scale_table = keep.tile([P, T], U8, name="scale_table", tag="scales_then_wt", align_bytes=64)
        for a, b in ((0, SCALE_AT), (SCALE_AT + BLOCKS, P)):
            nc.gpsimd.memset(scale_table[a:b, :].bitcast(I32), 0)
        x_scale = keep.tile([P, S], U8, name="x_scale", align_bytes=64)
        nc.vector.memset(x_scale[:].bitcast(I32), 0)
        nc.scalar.dma_start(scale_table[SCALE_AT : SCALE_AT + BLOCKS, :].bitcast(I32), x_scales[0].bitcast(I32))
        nc.sync.dma_start(offs_sb[:], offs)

        warm_in = spare.tile([P, 1], F32, name="warm_in")
        nc.gpsimd.memset(warm_in[:], 0.0)

        word_table = keep.tile([P, T], U32, name="word_table", tag="words_then_w2", align_bytes=64)
        nc.sync.dma_start(word_table[:].bitcast(I32), x_words[0].rearrange("p n r -> p (n r)").bitcast(I32))
        w1_rows = w1.rearrange("(p j) c -> p j c", j=PACK)
        w1_raw = keep.tile([P, PACK, H], F32, name="w1_raw")
        for a, b in ((0, 2), (2, 3), (3, 4)):
            nc.sync.dma_start(w1_raw[:, a:b, :], w1_rows[:, a:b, :])
        nc.sync.dma_start(take_sb[:], take)

        picked_scale = keep.tile([P, S], U8, name="picked_scale", align_bytes=64)
        by_vector(picked_scale[:], scale_table[:].indirect(offs_sb[:]))
        for q in range(4):
            rows = slice(SCALE_AT + 4 * q, SCALE_AT + 4 * q + 4)
            nc.scalar.dma_start(x_scale[32 * q : 32 * q + 4, :].bitcast(I32), picked_scale[rows, :].bitcast(I32))
        wt_sb = keep.tile([P, V], F32, name="wt_sb", tag="scales_then_wt", align_bytes=64)
        nc.sync.dma_start(wt_sb[:], wt.rearrange("(p j) v -> p j v", j=PACK)[:, 0, :])

        x_codes = keep.tile([P, S], U32, name="x_codes", align_bytes=64)
        by_vector(x_codes[:], word_table[:].indirect(offs_sb[:]))
        w2_raw = keep.tile([P, PACK, N], F32, name="w2_raw", tag="words_then_w2", align_bytes=64)
        for a in (0, HALF):
            nc.sync.dma_start(w2_raw[:, :, a : a + HALF], w2.rearrange("(p j) c -> p j c", j=PACK)[:, :, a : a + HALF])

        w1_cols = w1_raw[:].rearrange("p j (m u e) -> p e m u j", u=2, e=2)
        w1_codes = {e: keep.tile([P, H // 2], U32, name=f"w1_codes{e}", align_bytes=64) for e in (1, 0)}
        w1_scale = {e: keep.tile([P, H // 2], U8, name=f"w1_scale{e}", align_bytes=64) for e in (1, 0)}

        odd = keep.tile([P, 2, P, PACK], BF16, name="w1_odd", align_bytes=64)
        odd_cols = odd[:].rearrange("p u m j -> p m u j")
        by_vector(odd_cols[:, :, :, 0:2], w1_cols[:, 1, :, :, 0:2])
        by_vector(odd_cols[:, :, :, 2], w1_cols[:, 1, :, :, 2])
        for u in range(2):
            by_vector(odd_cols[:, :, u, 3], w1_cols[:, 1, :, u, 3])
        for u in range(2):
            quantize(w1_codes[1][:, u * P : (u + 1) * P], w1_scale[1][:, u * P : (u + 1) * P], odd[:, u, :, :])

        warm_gelu = spare.tile([P, 1], F32, name="warm_gelu")
        nc.scalar.activation(warm_gelu[:], warm_in[:], GELU)

        even = keep.tile([P, 2, P, PACK], BF16, name="w1_even", align_bytes=64)
        for a, b in ((0, 2), (2, 4)):
            by_scalar(even[:].rearrange("p u m j -> p m u j")[:, :, :, a:b], w1_cols[:, 0, :, :, a:b])
        quantize(w1_codes[0][:], w1_scale[0][:], even[:].rearrange("p u m j -> p (u m) j"))

        def new_bank():
            return psum.tile([P, S], F32, name="bank")

        def first_product(t, parts):
            cols, width, made = slice((t // 2) * P, (t // 2 + 1) * P), S // parts, []
            for a in range(0, S, width):
                tokens = slice(a, a + width)
                values = new_bank()[:, 0:width]
                multiply(values, w1_codes[t % 2][:, cols], w1_scale[t % 2][:, cols], x_codes[:, tokens], x_scale[:, tokens])
                made.append((values, tokens))
            return made

        y = {t: first_product(t, parts) for t, parts in ((1, 4), (3, 2), (0, 1), (2, 1))}

        pairs = [keep.tile([P, 2, S], F32, name=f"pair{u}") for u in range(2)]
        window = {}
        for u in range(2):
            window[2 * u] = pairs[u][:].rearrange("p s c -> p (s c)")
            window[2 * u + 1] = keep.tile([P, S], F32, name=f"single{u}", align_bytes=64)[:]
        z_codes = keep.tile([P, S], U32, name="z_codes", align_bytes=64)
        z_scale = keep.tile([P, S], U8, name="z_scale", align_bytes=64)

        def fill_window(t, copy, parts=slice(None)):
            for values, tokens in y[t][parts]:
                copy(window[t][:, tokens], values)

        def activate(t):
            done = keep.tile([P, S], F32, name=f"activated{t}", align_bytes=64)
            for values, tokens in y[t]:
                nc.scalar.activation(done[:, tokens], values, GELU)
            return done

        def fetch_weighted(t, activated, pool, **place):
            got = pool.tile([P, V], F32, name=f"weighted{t}", align_bytes=64, **place)
            nc.vector.tensor_tensor(got[:], activated[:].indirect(take_sb[:]), wt_sb[:], MULT)
            return got

        def scatter_by_vector(t, values):
            by_vector(window[t].indirect(take_sb[:]), values[:])

        def scatter_by_scalar(t, values):
            nc.scalar.activation(window[t].indirect(take_sb[:]), values[:], COPY)

        def group_w2(h, behind):
            grouped = keep.tile([P, HALF, PACK], BF16, name=f"w2_grouped{h}", tag=behind, align_bytes=64)
            rows = w2_raw[:, :, h * HALF : (h + 1) * HALF]
            nc.gpsimd.tensor_scalar(grouped[:], rows.rearrange("p j c -> p c j"), 1.0, 0.0, MULT, ADD)
            return grouped

        activated1 = activate(1)
        fill_window(1, by_vector, slice(0, 3))
        weighted1 = fetch_weighted(1, activated1, keep)
        weighted3 = fetch_weighted(3, activate(3), keep)
        weighted0 = fetch_weighted(0, activate(0), keep)
        fill_window(1, by_scalar, slice(3, 4))
        fill_window(3, by_scalar)

        scatter_by_vector(1, weighted1)
        w2_grouped = [group_w2(0, "activated0")]
        fill_window(0, by_vector)
        by_vector(pairs[0][:, 1, :], window[1])
        activated2 = activate(2)
        scatter_by_scalar(3, weighted3)

        weighted2 = fetch_weighted(2, activated2, placed, offset=3 * SLOT // 2)
        fill_window(2, by_scalar)
        by_scalar(pairs[1][:, 1, :], window[3])
        scatter_by_scalar(2, weighted2)
        w2_grouped.append(group_w2(1, "activated2"))
        scatter_by_vector(0, weighted0)

        w2_scale = keep.tile([P, N], U8, name="w2_scale", align_bytes=64)
        w2_codes, z_grouped = [], {}

        def quantize_w2(h, pool, **place):
            w2_codes.append(pool.tile([P, HALF], U32, name=f"w2_codes{h}", align_bytes=64, **place))
            quantize(w2_codes[h][:], w2_scale[:, h * HALF : (h + 1) * HALF], w2_grouped[h][:])

        def new_range(r, slot):
            z_grouped[r] = placed.tile([P, P, PACK], BF16, name=f"z_grouped{r}", offset=slot * SLOT, align_bytes=64)

        def group_z(copy, u, r):
            copy(z_grouped[r][:, :, 2 * u : 2 * u + 2], pairs[u][:, :, r * P : (r + 1) * P].rearrange("p s c -> p c s"))

        def quantize_z(r):
            quantize(z_codes[:, r * P : (r + 1) * P], z_scale[:, r * P : (r + 1) * P], z_grouped[r][:])

        quantize_w2(0, keep, tag="weighted0")
        new_range(0, 0)
        group_z(by_vector, 0, 0)
        group_z(by_vector, 1, 0)
        new_range(1, 1)
        group_z(by_vector, 0, 1)
        group_z(by_scalar, 1, 1)
        new_range(2, 2)
        group_z(by_scalar, 0, 2)
        group_z(by_scalar, 1, 2)
        quantize_z(0)
        quantize_z(1)
        quantize_w2(1, placed, offset=0)
        new_range(3, 1)
        group_z(by_vector, 0, 3)
        group_z(by_vector, 1, 3)
        quantize_z(2)
        quantize_z(3)

        out_rows = out.rearrange("(mt p) j -> p mt j", p=P)

        def result(mt, cuts, copy):
            bank, first, width = new_bank(), cuts[0], cuts[-1] - cuts[0]
            weights = w2_codes[mt // 2][:, mt % 2 * P : (mt % 2 + 1) * P]
            for a, b in zip(cuts, cuts[1:]):
                multiply(bank[:, a - first : b - first], weights, w2_scale[:, mt * P : (mt + 1) * P], z_codes[:, a:b], z_scale[:, a:b])
            staged = keep.tile([P, width], F32, name=f"staged{mt}_{first}")
            copy(staged[:], bank[:, 0:width])
            nc.sync.dma_start(out_rows[:, mt, first : first + width], staged[:])

        result(0, (0, P), by_scalar)
        result(0, (P, HALF), by_scalar)
        result(1, (0, P, HALF), by_scalar)
        result(2, (0, HALF), by_scalar)
        result(3, (0, HALF), by_scalar)
        result(0, (HALF, HALF + P, S), by_vector)
        result(1, (HALF, S), by_scalar)
        result(2, (HALF, S), by_vector)
        staged = keep.tile([P, HALF], F32, name="staged_last")
        for i, copy in enumerate((by_vector, by_scalar)):
            bank, tokens = new_bank(), slice(HALF + i * P, HALF + (i + 1) * P)
            multiply(bank[:, 0:P], w2_codes[1][:, P:HALF], w2_scale[:, N - P : N], z_codes[:, tokens], z_scale[:, tokens])
            copy(staged[:, i * P : (i + 1) * P], bank[:, 0:P])
        nc.sync.dma_start(out_rows[:, 3, HALF:S], staged[:])
